import numpy as np, ml_dtypes
CORES = [40,64,80,88,96,104,120,144]
N = 8
import mx_ref
BF = ml_dtypes.bfloat16
def gentries(a):
    return np.ascontiguousarray(a.reshape(8, 16, -1).transpose(0, 2, 1)).reshape(8, -1)
def gtable(e):
    e = np.asarray(e); return np.ascontiguousarray(e.reshape(8, -1, 16).transpose(0, 2, 1)).reshape(128, -1).astype(np.int32)
def gcols(t, e):
    v = np.concatenate([t.reshape(8, 16, -1, 4), np.zeros((8, 16, 1, 4), BF)], axis=2)
    return np.ascontiguousarray(np.stack([v[g][:, e[g]] for g in range(8)])).reshape(128, -1)
def tile(rs):
    return np.stack(rs, axis=2).reshape(128, -1).astype(BF)
def cut(t, i, w=512):
    return t[:, w * i:w * i + w]
def pick(q, e):
    c = np.concatenate([q[0].reshape(128, -1, 4), np.zeros((128, 1, 4), np.uint8)], axis=1); s = np.concatenate([q[1], np.ones((16, 1), np.uint8)], axis=1)
    return (np.ascontiguousarray(c[:, e].reshape(128, -1)), np.ascontiguousarray(s[:, e]))
def join(*qs):
    return (np.concatenate([q[0] for q in qs], axis=1), np.concatenate([q[1] for q in qs], axis=1))
def put(q, e, v):
    c, s = q[0].reshape(128, -1, 4).copy(), q[1].copy(); c[:, e] = v[0].reshape(128, -1, 4); s[:, e] = v[1]
    return (c.reshape(128, -1), s)
def pk(c, s):
    return (np.ascontiguousarray(c), mx_ref.live(s))
def emit(q):
    return q[0], q[1]
def packed(v, rng):
    q = [mx_ref.quantize(np.ascontiguousarray(v[r])) for r in range(N)]
    return np.stack([a for a, b in q]), np.stack([mx_ref.plane(b, rng) for a, b in q])
def values_of_codes():
    e, c = np.zeros((128, 128, 4), np.float32), np.zeros((128, 2, 4), np.uint8)
    e[np.arange(128), np.arange(128), 0] = 1
    c[:127, :, 0] = np.arange(256).reshape(2, 128).T[:127]
    return mx_ref.matmul(mx_ref.quantize(e.reshape(128, 512).astype(BF)), (c.reshape(128, 8), np.full((16, 2), 127, np.uint8))).T.reshape(-1).astype(np.float64)
CODE_VALUE, SCALE_VALUE = values_of_codes(), 2.0 ** (np.arange(256) - 127.0)
def decode(q):
    return (CODE_VALUE[q[0]].reshape(16, 8, -1, 4) * SCALE_VALUE[q[1]][:, None, :, None] + 0.0).reshape(128, -1).astype(np.float32)
def f(rng, *shape):
    return mx_ref.flush((rng.standard_normal(shape, dtype=np.float32) * np.exp2(rng.integers(-2, 3, shape[:-1] + (1,)))).astype(BF))
def wide(rng, *shape, cols=0):
    v = rng.standard_normal(shape, dtype=np.float32) * np.exp2(rng.integers(-12, 13, shape)).astype(np.float32)
    if cols: v *= np.repeat(np.exp2(rng.integers(-cols, cols + 1, shape[:-2] + (1, shape[-1] // 4))) * (rng.random(shape[:-2] + (1, shape[-1] // 4)) > 0.0625), 4, axis=-1).astype(np.float32)
    return mx_ref.flush(v.astype(BF))
C, V, B, R = 352, 11, 32, 3
def big(v):
    v = v.astype(np.float32)
    v[np.abs(v) < np.float32(2.0 ** -16)] = 0
    return v.astype(BF)
def numbers_of(rng):
    return {"x": big(f(rng, N, 128, 4 * C)), "u": np.array(f(rng, N, 128, 512)), "v": np.array(f(rng, N, 128, 512))}
def weights(rng, still=[]):
    w = big(f(rng, N, 128, 2048)).reshape(N, 8, 16, 4, 8, 16, 4)
    for i in still:
        w[:, :, i] = 0
        w[:, :, :, :, :, i] = 0
    c, p = packed(w.reshape(N, 128, 2048), rng)
    return {"wc": c, "ws": p}
def yards(h, p):
    return {"hg": np.stack([gtable(h[r].reshape(8, 3 * B)) for r in range(N)]), "dg": np.stack([gtable(p[r]) for r in range(N)])}
def heights(rng):
    c = np.sort(rng.integers(0, V + 1, (N, 8, 2, B)), axis=2)
    return np.concatenate([c[:, :, :1], c[:, :, 1:] - c[:, :, :1], V - c[:, :, 1:]], axis=2)
def deals(rng):
    return np.argsort(rng.random((N, 8, C)), axis=2)
def signs(rng):
    return np.stack([rng.permutation(8) % 2 * 2.0 - 1.0 for r in range(N)])
def setup_inputs(rng):
    return {**numbers_of(rng), **weights(rng), **yards(heights(rng), deals(rng))}
def setup_inputs_ties(rng):
    d = numbers_of(rng)
    e = rng.permutation(N)
    x = d["x"].reshape(N, 8, 16, C, 4)
    for r in range(N):
        k = np.zeros(C, int) if r == e[0] else rng.permutation(C) % 3
        a = x[r][:, :8, :3].copy()
        a[:, :, 2] = 0
        x[r][:, :8] = a[:, :, k]
    x[e[1]] = 0
    u = d["u"].reshape(N, 8, 16, 8, 16, 4)
    k = u.copy()
    u[:, :, :, :, 0] = 0
    for g in range(8): u[:, g, :8, g, 0] = k[:, g, :8, g, 0]
    return {"x": x.reshape(N, 128, 4 * C), "u": u.reshape(N, 128, 512), "v": d["v"], **weights(rng, range(8)), **yards(heights(rng), deals(rng))}
def setup_inputs_near(rng):
    d = numbers_of(rng)
    x = d["x"].astype(np.float32).reshape(N, 8, 16, C, 4)
    u = d["u"].reshape(N, 128, 128, 4)
    x[:, :, 0] = 0
    u[:, :, ::16] = 0
    o, c = rng.permutation(N) % 4, signs(rng)
    for r in range(N):
        t = (V - 1 - (np.arange(V) + rng.integers(0, V, (8, B, 1))) % V).reshape(8, C)
        s = t // 2
        size = 1.0 if o[r] < 2 else 2.0 ** -4
        if o[r] < 2:
            x[r, :, 0, :, 0] = c[r][:, None]
            for i in rng.permutation(8)[:4]: x[r, i, 0, rng.integers(C), 0] *= np.float32(2.0 ** 30)
        if o[r] == 3:
            x[r, :, 1:8] = 0
            x[r, :, 0, :, 0] = (8 + t % 2) * 2.0 ** -30
        x[r, :, 8] = ((s[:, :, None] >> np.arange(4)) & 1) * np.exp2(np.arange(4) - 23.0) * size
        x[r, :, 9:] = rng.integers(4, 8, (8, 7, C, 4)) * 2.0 ** -20 * size
        k = 1.0 if o[r] == 0 else 2.0 ** -30
        for h in range(0, 128, 16):
            u[r, h, h, 0] = k
            u[r, h + 8, h] = k
    return {"x": x.reshape(N, 128, 4 * C).astype(BF), "u": u.reshape(N, 128, 512), "v": d["v"], **weights(rng, [0, 8, 9, 10, 11, 12, 13, 14, 15]), **yards(heights(rng), deals(rng))}
def setup_inputs_stacks(rng):
    d = numbers_of(rng)
    x = d["x"].reshape(N, 8, 16, C, 4)
    u = d["u"].reshape(N, 128, 128, 4)
    h, s = np.zeros((N, 8, 3, B), int), rng.integers(4, 8, (N, 8, B, V))
    for r in range(N):
        for g in range(8):
            c = rng.permutation(B) % 6
            for i in range(B):
                a, l, o = rng.permutation(3)
                m = int(rng.integers(1, V - 2))
                w = np.zeros(3, int)
                w[[a, l, o]] = [(V, 0, 0), (V, 0, 0), (1, V - 1, 0), (V - 2, 0, 2), (V - 2, 1, 1), (2, m, V - 2 - m)][c[i]]
                h[r, g, :, i] = w
                b = [0, w[0], w[0] + w[1]]
                k = s[r, g, i]
                k[b[a] + (V - 1 if c[i] == 1 else 0)] = 1
                if c[i] == 4: k[b[l]] = k[b[o]]
                if c[i] == 5: k[b[o] + rng.integers(w[o])] = 2
    s[rng.permutation(N) < N // 2] -= 12
    x[:, :, 0] = 0
    x[:, :, 0, :, 0] = s.reshape(N, 8, C).astype(np.float32).astype(BF)
    u[:, :, ::16] = 0
    for j in range(0, 128, 16): u[:, j, j, 0] = 1
    p, e = deals(rng), rng.permutation(N)
    p[e[0]] = np.arange(C)
    p[e[1]] = np.arange(C)[::-1]
    return {"x": x.reshape(N, 128, 4 * C), "u": u.reshape(N, 128, 512), "v": d["v"], **weights(rng, [0]), **yards(h, p)}
def setup_inputs_huge(rng):
    d = numbers_of(rng)
    x = 2.0 ** 30 * (0.8 + 0.2 * rng.random((N, 128, C, 4)))
    c = np.stack([rng.permutation(C) % 2 * 2.0 - 1.0 for r in range(N)])
    c[rng.permutation(N) < N // 2] = 1
    x *= c[:, None, :, None]
    u = d["u"].reshape(N, 128, 128, 4)
    a = 2.0 ** 30 * (1 - 0.1 * rng.random((N, 128, 8, 4))) * signs(rng)[:, None, :, None]
    u[:, :, ::16] = a.astype(np.float32).astype(BF)
    w = np.zeros((N, 128, 4, 128, 4), np.float32)
    i = np.arange(128)
    for b in range(4): w[:, i, b, i, b] = -1
    wc, ws = packed(w.reshape(N, 128, 2048).astype(BF), rng)
    return {"x": x.astype(np.float32).reshape(N, 128, 4 * C).astype(BF), "u": u.reshape(N, 128, 512), "v": d["v"], "wc": wc, "ws": ws, **yards(heights(rng), deals(rng))}
def setup_inputs_spread(rng):
    d = setup_inputs(rng)
    d["x"] = big(wide(rng, N, 128, 4 * C, cols=6))
    return d
def check_inputs(d):
    b = []
    for k in ("x", "u", "v"):
        a = np.abs(d[k].astype(np.float32))
        if not (np.isfinite(a).all() and ((a == 0) | (a >= 2.0 ** -30) & (a <= 2.0 ** 30)).all()): b.append("a value of " + k)
    if ((d["wc"] & 0x7F) == 0x7F).any(): b.append("a code of wc that is no number")
    none, least, most = [emit(mx_ref.quantize(np.full((128, 16), k, np.float32).astype(BF)))[1][0, 0] for k in (0.0, 2.0 ** -30, 2.0 ** 30)]
    for r in range(N):
        s = mx_ref.live(d["ws"][r])
        if ((s != none) & ((s < least) | (s > most))).any(): b.append("a scale of ws")
        h = gentries(d["hg"][r]).reshape(8, 3, B)
        if (h < 0).any() or (h > V).any() or (np.sum(h, axis=1) != V).any(): b.append("the heights hg")
        if (np.sort(gentries(d["dg"][r]), axis=1) != np.arange(C)).any(): b.append("dg: no permutation")
    return b
def reference(x, u, v, wc, ws, hg, dg):
    qu = [mx_ref.quantize(u[r]) for r in range(N)]
    lay = [pk(wc[r], ws[r]) for r in range(N)]
    now = [x[r] for r in range(N)]
    high = [gentries(hg[r]).reshape(8, 3, B).transpose(0, 2, 1) for r in range(N)]
    place, three, start = np.arange(V), np.arange(3), V * np.arange(B)[:, None]
    for t in range(R):
        sent, moved = [], []
        for r in range(N):
            s = (mx_ref.matmul(qu[r], mx_ref.quantize(now[r]))[::16] + np.float32(0.0)).reshape(8, B, V)
            h = high[r]
            end = np.stack([h[:, :, 0], h[:, :, 0] + h[:, :, 1], np.full((8, B), V)], axis=2)
            stack = (place >= end[:, :, :1]).astype(int) + (place >= end[:, :, 1:2])
            k = np.argmin(s, axis=2)[:, :, None]
            a = np.take_along_axis(stack, k, axis=2)
            low = np.stack([np.min(np.where(stack == i, s, np.float32(np.inf)), axis=2) for i in range(3)], axis=2)
            low[three == a] = -np.inf
            l = np.argmax(low, axis=2)[:, :, None]
            up = (stack == a) & (place > k)
            m = np.where(up & (np.take_along_axis(h, l, axis=2) > 0), np.take_along_axis(end, l, axis=2) - 1, place)
            key = np.where(up, 4 * V * l + 2 * V - place, 4 * V * stack + place)
            key = np.where(place == k, 4 * V * a + 3 * V, key)
            o = np.argsort(key, axis=2)
            high[r] = h + np.sum(up, axis=2)[:, :, None] * ((three == l).astype(int) - (three == a).astype(int))
            moved.append(((start + o).reshape(8, C), (start + np.take_along_axis(m, o, axis=2)).reshape(8, C), (o == k).reshape(8, C)))
            sent.append(mx_ref.quantize(gcols(now[r], (start + k).reshape(8, B))))
        came = decode(join(*sent)).astype(BF)
        for r in range(N):
            c = np.ascontiguousarray(cut(came, (r - 1) % N, 4 * B))
            q = mx_ref.quantize(c)
            new = tile([mx_ref.matmul(pick(lay[r], np.arange(128 * b, 128 * b + 128)), q) * np.float32(0.015625) + c[:, b::4].astype(np.float32) for b in range(4)])
            e, m, arrived = moved[r]
            z = ((gcols(now[r], e).astype(np.float32) + gcols(now[r], m).astype(np.float32)) * np.float32(0.5)).astype(BF)
            yard = np.where(arrived, C + np.arange(C) // V, np.arange(C))
            now[r] = gcols(np.concatenate([z, new], axis=1), np.take_along_axis(yard, gentries(dg[r]), axis=1))
    y, oh = np.zeros((N, 128, C), np.float32), np.zeros((N, 8, 3 * B), np.float32)
    oc, osc = np.zeros((N, 128, 4 * C), np.uint8), np.zeros((N, 16, C), np.uint8)
    for r in range(N):
        q = mx_ref.quantize(now[r])
        y[r] = mx_ref.matmul(mx_ref.quantize(v[r]), q)
        oh[r] = high[r].transpose(0, 2, 1).reshape(8, 3 * B)
        oc[r], osc[r] = emit(q)
    return {"y": y, "oh": oh, "oc": oc, "osc": osc}

@@ -1,0 +1,588 @@
+from concourse.bass import DstId, RemoteDMATransfer
+from concourse.mybir import dt, AluOpType, AxisListType, ActivationFunctionType
+
+C, V, B, ROUNDS = 352, 11, 32, 3
+XA, XX, XG = 0, 128, 128 + 4 * C
+PL = C + B
+BIG, TOP = 2.0 ** 90, 2.0 ** 80
+
+F32, BF, I32, U16, CODE, PLANE = "float32", "bfloat16", "int32", "uint16", "float8_e4m3fn_x4", "uint8"
+
+
+def _sb(n, d):
+    return ("sbuf", [128, n], d)
+
+
+SCRATCH = {
+    "xin": _sb(4 * C, BF), "xb": _sb(XG + 128, BF), "zz": _sb(4 * PL, BF), "xp": _sb(4 * C, BF),
+    "ub": _sb(512, BF), "vb": _sb(512, BF), "et": _sb(516, BF), "c64": _sb(516, BF),
+    "qu": _sb(128, CODE), "su": _sb(128, PLANE), "qur": _sb(128, CODE), "sur": _sb(128, PLANE),
+    "qv": _sb(128, CODE), "sv": _sb(128, PLANE), "qw": _sb(512, CODE), "sw": _sb(512, PLANE),
+    "qe": _sb(512, CODE), "se": _sb(512, PLANE), "qx": _sb(C, CODE), "sx": _sb(C, PLANE),
+    "qg": _sb(128, CODE), "sg": _sb(128, PLANE),
+    "hgi": _sb(6, I32), "dgi": _sb(22, I32), "pi": _sb(2, I32), "pj": _sb(2, I32), "ti": _sb(22, I32), "fi": _sb(2, I32),
+    "col": _sb(16, F32), "i32": _sb(32, F32), "i44": _sb(44, F32), "sm": _sb(64, F32), "tab": _sb(PL, F32),
+    "m16": _sb(16, F32), "r16": _sb(16, F32), "x16": _sb(48, F32),
+    "maskq": _sb(C, F32), "rst": _sb(C, F32), "cex": _sb(C, F32),
+    "bb": _sb(C, F32), "sc": _sb(C, F32), "r22": _sb(22, F32), "mm": _sb(22, F32), "gt": _sb(24, F32),
+    "ca": _sb(8, F32), "kp": _sb(22, F32), "kn": _sb(11, F32), "k05": _sb(16, F32), "de": _sb(64, F32), "dp": _sb(32, F32),
+    "m3": _sb(96, F32), "s3": _sb(96, F32), "ls": _sb(96, F32), "pm": _sb(8, F32),
+    "ind": _sb(16, F32), "eu": _sb(8 * (ROUNDS + 1), F32), "pr": _sb(16, F32), "es": _sb(16, F32), "c4": _sb(16, F32),
+    "par": _sb(8, F32), "stp": _sb(8, F32), "cof": _sb(8, F32), "dl": _sb(8, F32), "vc": _sb(2, F32),
+    "ys": _sb(96, F32), "cofc": _sb(96, F32), "ch": _sb(96, F32), "st1": _sb(96, F32), "st2": _sb(96, F32),
+    "st3": _sb(96, F32), "st4": _sb(96, F32), "yi": _sb(24, F32), "yb": _sb(24, F32), "ef": _sb(24, F32),
+    "cl": _sb(22, F32), "vv": _sb(22, F32), "eq": _sb(22, F32), "wm": _sb(22, F32), "mf": _sb(22, F32),
+    "bi": _sb(22, F32), "bm": _sb(22, F32),
+    "d1": _sb(22, F32), "d2": _sb(22, F32), "d3": _sb(22, F32), "d4": _sb(22, F32), "d5": _sb(22, F32), "d6": _sb(22, F32),
+    "i1": _sb(PL, F32), "i2": _sb(C, F32), "i3": _sb(C, F32), "ex": _sb(C, F32),
+    "hf": _sb(8, F32), "ho": _sb(32, F32), "ht": _sb(32, F32), "ysb": _sb(C, F32),
+    "offp": _sb(44, U16), "offq": _sb(22, U16), "offu": _sb(8, U16), "offn": _sb(22, U16), "offa": _sb(8, U16),
+    "off3": _sb(6, U16), "offs": _sb(6, U16), "offc": _sb(6, U16), "offe": _sb(24, U16),
+    "offd": _sb(22, U16), "offm": _sb(22, U16), "offf": _sb(22, U16),
+    "ps": ("psum", [128, 4096], F32),
+}
+for _t in range(ROUNDS):
+    SCRATCH["qa%d" % _t] = _sb(160, CODE)
+    SCRATCH["sa%d" % _t] = _sb(256, PLANE)
+
+NDMA = 26
+ENGSEM = {"v": "cv", "s": "cs", "p": "cp", "g": "cg"}
+SEMAPHORES = ["cv", "cs", "cp", "cg", "sent"] + ["arr%d" % t for t in range(ROUNDS)] + ["dma%d" % i for i in range(NDMA)]
+
+
+def helpers(src, dst, T, topo):
+    if topo.may_write(src, dst):
+        return []
+    near = [c for c in topo.cores_of(src) if c != src and T.rank_of(c) is None and topo.may_write(c, dst)]
+    near.sort(key=lambda c: (topo.die(c) != topo.die(src), c))
+    return near[:2]
+
+
+def bits(engines):
+    m = 0
+    for e in engines:
+        m |= 1 << e
+    return m
+
+
+def relay_program(g, core, T, topo):
+    n = len(T.cores)
+    for r in range(n):
+        src, dst = T.cores[r], T.cores[(r + 1) % n]
+        hs = helpers(src, dst, T, topo)
+        if core not in hs:
+            continue
+        rid, pid = topo.addr(dst, core)
+        came = len(topo.engines(src, core)) // 2
+        eng = topo.engines(core, dst)
+        for t in range(ROUNDS):
+            g.wait_ge(T.sem["arr%d" % t], came)
+            if core == hs[0]:
+                piece = T["qa%d" % t][:, 128:160].bitcast(dt.uint8)
+            else:
+                piece = T["sa%d" % t][:, 128:160]
+            g.remote_dma(piece, piece, T.sem["arr%d" % t], T.sem.sent, pid, rid, bits(eng))
+        g.wait_ge(T.sem.sent, ROUNDS * len(eng))
+
+
+def rank_program(g, core, T, topo):
+    rank = T.rank_of(core)
+    if rank is None:
+        relay_program(g, core, T, topo)
+        return
+    n = len(T.cores)
+    nxt, prv = T.cores[(rank + 1) % n], T.cores[(rank - 1) % n]
+    queue = {"v": g.vector, "s": g.scalar, "p": g.tensor, "g": g, "y": g.sync}
+    alu, act = AluOpType, ActivationFunctionType
+
+    def W(name, a=0, b=None, step=1, p0=0, p1=128):
+        return (name, a, SCRATCH[name][1][1] if b is None else b, step, p0, p1)
+
+    def ap(v):
+        name, a, b, step, p0, p1 = v
+        rows = slice(p0, p1) if (p0, p1) != (0, 128) else slice(None)
+        return T[name][rows, a:b:step] if step != 1 else T[name][rows, a:b]
+
+    def cover(v):
+        name, a, b, step = v[:4]
+        if name == "ps":
+            return 1 << (a // 512)
+        if step == 1:
+            return ((1 << (b - a)) - 1) << a
+        m = 0
+        for i in range(a, b, step):
+            m |= 1 << i
+        return m
+
+    touched = {}
+    known = {q: {} for q in queue}
+    count = {q: 0 for q in ENGSEM}
+    dmas = [0]
+
+    def learn(q, sem, val, clock):
+        if known[q].get(sem, 0) >= val:
+            return
+        queue[q].wait_ge(T.sem[sem], val)
+        known[q][sem] = val
+        for s2, v2 in clock.items():
+            if known[q].get(s2, 0) < v2:
+                known[q][s2] = v2
+
+    def issue(q, call, reads, writes, dma=False, chained=False):
+        need = []
+        for views, wr in ((reads, False), (writes, True)):
+            for v in views:
+                m = cover(v)
+                for (m2, wr2, q2, sem, val, clock) in touched.get(v[0], []):
+                    if not m & m2:
+                        continue
+                    if v[0] == "ps":
+                        if q2 == q and (chained or not (wr or wr2)):
+                            continue
+                    elif not (wr or wr2):
+                        continue
+                    need.append((sem, val, clock))
+        need.sort(key=lambda e: -e[1])
+        for sem, val, clock in need:
+            learn(q, sem, val, clock)
+        ins = call()
+        if dma:
+            sem, val = "dma%d" % dmas[0], 16
+            dmas[0] += 1
+            ins.then_inc(T.sem[sem], 16)
+        else:
+            count[q] += 1
+            sem, val = ENGSEM[q], count[q]
+            ins.then_inc(T.sem[sem], 1)
+        clock = dict(known[q])
+        for views, wr in ((reads, False), (writes, True)):
+            for v in views:
+                m = cover(v)
+                old = touched.setdefault(v[0], [])
+                if wr:
+                    old[:] = [e for e in old if e[0] & ~m]
+                old.append((m, wr, q, sem, val, clock))
+
+    def await_writes(q, v):
+        for (m2, wr2, q2, sem, val, clock) in touched[v[0]]:
+            if wr2 and m2 & cover(v):
+                learn(q, sem, val, clock)
+
+    def src(v):
+        if len(v) == 2:
+            return ap(v[0]).indirect(ap(v[1])), [v[0], v[1]]
+        return ap(v), [v]
+
+    def scal(s):
+        return (ap(s), [s]) if isinstance(s, tuple) else (s, [])
+
+    def memset(o, c):
+        issue("v", lambda: g.vector.memset(ap(o), c), [], [o])
+
+    def copy(o, i):
+        a, r = src(i)
+        issue("v", lambda: g.vector.tensor_copy(ap(o), a), r, [o])
+
+    def tt(o, i0, i1, op):
+        a, r = src(i0)
+        issue("v", lambda: g.vector.tensor_tensor(ap(o), a, ap(i1), op), r + [i1], [o])
+
+    def ts(o, i0, s1, op0, s2=None, op1=None):
+        a, r = src(i0)
+        x1, r1 = scal(s1)
+        x2, r2 = scal(s2)
+        if op1 is None:
+            issue("v", lambda: g.vector.tensor_scalar(ap(o), a, x1, None, op0), r + r1, [o])
+        else:
+            issue("v", lambda: g.vector.tensor_scalar(ap(o), a, x1, x2, op0, op1), r + r1 + r2, [o])
+
+    def scan(o, d0, d1, init, op0, op1):
+        issue("v", lambda: g.vector.tensor_tensor_scan(ap(o), ap(d0), ap(d1), init, op0, op1), [d0, d1], [o])
+
+    def reduce(o, i, op):
+        issue("v", lambda: g.vector.tensor_reduce(ap(o), ap(i), AxisListType.X, op), [i], [o])
+
+    def quant(q, s, i):
+        issue("v", lambda: g.vector.quantize_mx(ap(q), ap(s), ap(i)), [i], [q, s])
+
+    def activ(o, i, func, scale=1.0, bias=0.0):
+        a, r = src(i)
+        x, r1 = scal(scale)
+        y, r2 = scal(bias)
+        issue("s", lambda: g.scalar.activation(ap(o), a, func, bias=y, scale=x), r + r1 + r2, [o])
+
+    def scaled(q, o, i, c):
+        if q == "v":
+            ts(o, i, c, alu.mult)
+        else:
+            activ(o, i, act.Identity, c)
+
+    def moved(q, o, i):
+        if q == "v":
+            copy(o, i)
+        else:
+            a, r = src(i)
+            issue("s", lambda: g.scalar.activation(ap(o), a, act.Copy), r, [o])
+
+    def mm(bank, ncol, wq, ws, xq, xs, start=True, stop=True):
+        o = W("ps", 512 * bank, 512 * bank + ncol)
+        issue("p", lambda: g.tensor.matmul_mx(ap(o), ap(wq), ap(ws), ap(xq), ap(xs), start, stop),
+              [wq, ws, xq, xs], [o], chained=not start)
+
+    def iota(o, pattern, base=0, cm=0):
+        if SCRATCH[o[0]][2] == I32:
+            issue("g", lambda: g.iota(ap(o), pattern, base, cm), [], [o])
+        else:
+            issue("g", lambda: g.iota(ap(o), pattern, base, cm, allow_small_or_imprecise_dtypes=True), [], [o])
+
+    def load(q, o, i, codes=False):
+        a = ap(o).bitcast(dt.uint8) if codes else ap(o)
+        issue(q, lambda: queue[q].dma_start(a, i), [], [o], dma=True)
+
+    def store(q, o, i, codes=False):
+        a = ap(i).bitcast(dt.uint8) if codes else ap(i)
+        issue(q, lambda: queue[q].dma_start(o, a), [i], [], dma=True)
+
+    def one(name, j):
+        return W(name, j, j + 1)
+
+    def pair(name, j):
+        return W(name, j, j + 5, 4)
+
+    half = 2 * C
+    load("y", W("ub"), T.u[:])
+    load("s", W("hgi"), T.hg[:])
+    load("y", W("xin", 0, half), T.x[:, 0:half])
+    load("s", W("dgi"), T.dg[:])
+    load("y", W("xin", half, 2 * half), T.x[:, half:2 * half])
+
+    Q, Q3, Q11, PP, Q4, QC, INV, FS = [one("col", j) for j in range(8)]
+    iota(W("pi"), [[0, 2]], 0, 1)
+    iota(W("i32"), [[0, 2], [1, 16]])
+    iota(W("i44"), [[4, 11], [176, 4]])
+    iota(W("sm", 0, 8), [[704, 2], [1, 4]], -64)
+    iota(W("sm", 8, 14), [[0, 3], [176, 2]], 15)
+    iota(W("sm", 18, 24), [[4, 2], [0, 3]])
+    iota(W("sm", 24, 46), [[176, 2], [1, 11]])
+    iota(W("yi"), [[176, 2], [16, 12]])
+    iota(W("bi"), [[16, 22]])
+    iota(W("eu"), [[0, 8 * (ROUNDS + 1)]])
+    iota(W("eu", 2, 8 * (ROUNDS + 1), 4), [[0, 2 * (ROUNDS + 1)]], V)
+    iota(W("gt"), [[0, 24]], 1)
+    iota(W("kp"), [[0, 2], [1, 11]], 1)
+    iota(W("kn"), [[-1, 11]], -1)
+    iota(W("ind"), [[0, 16]])
+    iota(W("ind", 0, 16, 4), [[0, 4]], 1)
+    iota(W("c4"), [[0, 16]], 1)
+    iota(W("c4", 0, 16, 4), [[0, 4]])
+    iota(W("stp"), [[0, 8]])
+    iota(W("ys"), [[0, 2], [1, 12], [0, 4]])
+    iota(W("ys", 1, 96, 4), [[0, 2], [1, 12]], 1)
+    iota(W("cofc", 1, 96, 4), [[10, 2], [0, 12]], -23)
+    iota(W("cofc", 2, 96, 4), [[10, 2], [0, 12]], -23)
+    iota(W("cofc", 0, 96, 4), [[0, 2], [-2, 12]], -1)
+    iota(W("cofc", 3, 96, 4), [[0, 2], [-2, 12]], -1)
+    iota(W("ch", 1, 96, 2), [[0, 48]], 1)
+    iota(W("ch", 0, 96, 2), [[0, 24], [-1, 2]])
+
+    memset(W("c64"), 64.0)
+    memset(W("r16"), -TOP)
+    ts(one("pj", 0), one("pi", 0), 15, alu.bitwise_and)
+    ts(one("pj", 1), one("pi", 1), 3, alu.bitwise_and)
+    memset(W("r16", 0, 1), TOP)
+    copy(W("col", 0, 2), W("pj"))
+    ts(W("offu"), W("i32", 0, 8), 16.0, alu.mult)
+    ts(W("offq"), W("i32", 0, 22), 0.0, alu.mult, Q, alu.add)
+    ts(W("m16"), W("i32", 0, 16), Q, alu.not_equal, BIG, alu.mult)
+    ts(Q11, Q, 11.0, alu.mult)
+    ts(W("x16", 0, 16), W("i32", 0, 16), Q, alu.not_equal)
+    moved("s", W("maskq"), (W("m16"), W("offq")))
+    moved("s", W("rst"), (W("r16"), W("offq")))
+    ts(W("x16", 16, 32), W("i32", 15, 31), Q, alu.is_equal, 1023.0, alu.mult)
+    ts(PP, Q3, -10.0, alu.mult, Q11, alu.add)
+    ts(Q4, Q, 4.0, alu.mult)
+    tt(W("x16", 32, 48), W("x16", 0, 16), W("x16", 16, 32), alu.add)
+    ts(W("offp"), W("i44"), PP, alu.add)
+    memset(W("r22"), -TOP)
+    ts(FS, Q3, 0.5, alu.mult, 0.25, alu.add)
+    ts(W("ca"), W("sm", 0, 8), Q4, alu.add, 1.0 / 64, alu.mult)
+    memset(W("r22", 0, 22, 11), TOP)
+    copy(one("fi", 0), FS)
+    ts(QC, Q, 10.0, alu.min, 16.0, alu.mult)
+    ts(W("k05"), W("i32", 0, 16), 10.0, alu.min, 0.5, alu.add)
+    copy(FS, one("fi", 0))
+    ts(W("off3"), W("sm", 8, 14), QC, alu.add)
+    ts(W("offc"), W("sm", 18, 24), Q3, alu.add)
+    ts(W("offs"), W("sm", 18, 24), FS, alu.add)
+    ts(INV, Q, 15.0, alu.is_equal, 1.0 / 1024, alu.max)
+    ts(W("offn"), W("sm", 24, 46), Q11, alu.add)
+    ts(W("yb"), W("yi"), Q, alu.add, 1.0 / 16, alu.mult)
+    ts(W("bm"), W("bi"), Q, alu.add)
+
+    dealing = [
+        lambda: ts(W("d2"), W("dgi"), -5.0, alu.add, 1.0 / V, alu.mult),
+        lambda: copy(W("ti"), W("d2")),
+        lambda: ts(W("d1"), W("dgi"), 16.0, alu.mult),
+        lambda: ts(W("d3"), W("ti"), -175.0, alu.mult),
+        lambda: ts(W("d4"), W("ti"), 16.0, alu.is_ge, 176.0, alu.mult),
+        lambda: tt(W("d5"), W("d1"), W("d3"), alu.add),
+        lambda: tt(W("d6"), W("d5"), W("d4"), alu.add),
+        lambda: copy(W("offd"), W("d6")),
+    ]
+
+    def filler(k=1):
+        for _ in range(k):
+            if dealing:
+                dealing.pop(0)()
+
+    def first_ends():
+        copy(W("hf", 0, 6), W("hgi"))
+        copy(pair("eu", 0), W("hf", 0, 2))
+        tt(pair("eu", 1), W("hf", 0, 2), W("hf", 2, 4), alu.add)
+
+    def end_gaps(t):
+        for e in range(2):
+            for h in range(2):
+                activ(W("de", 32 * e + 16 * h, 32 * e + 16 * h + 16), W("k05"), act.Identity, -1.0, one("eu", 8 * t + 4 * h + e))
+
+    def stack_masks():
+        activ(W("m3", 0, 32), W("de", 0, 32), act.Relu, -BIG)
+        activ(W("m3", 64, 96), W("de", 32, 64), act.Relu, BIG)
+        activ(W("m3", 32, 64), W("dp"), act.Relu, BIG)
+
+    XW = W("xb", XX, XG)
+
+    def quant_x(c0, c1):
+        quant(W("qx", c0, c1), W("sx", c0, c1), W("xb", XX + 4 * c0, XX + 4 * c1))
+
+    def hide(bank, c0, c1):
+        tt(W("bb", c0, c1), W("ps", 512 * bank, 512 * bank + c1 - c0), W("maskq", c0, c1), alu.add)
+
+    def own(c0, c1):
+        scan(W("sc", c0, c1), W("rst", c0, c1), W("bb", c0, c1), 0.0, alu.max, alu.min)
+
+    def order_x(q, h, part):
+        a = XX + half * h + C * part
+        moved(q, W("xb", a, a + C), (W("xin", half * h, half * h + half), W("offp", 22 * part, 22 * part + 22)))
+
+    def deal(q, t, s0, s1):
+        scaled(q, W("xb", XX + 64 * s0 + t, XX + 64 * s1, 4),
+               (W("zz", PL * t, PL * t + PL), W("offf", s0, s1)), 0.5)
+
+    def plane(k):
+        moved("s", W("xp", C * k, C * k + C), W("xb", XX + k, XG, 4))
+
+    def both(k):
+        tt(W("zz", PL * k, PL * k + C), (W("xp", C * k, C * k + C), W("offm")), W("xb", XX + k, XG, 4), alu.add)
+
+    K1 = [one("cof", 4 * h + 1) for h in range(2)]
+    NN = [one("par", 4 * h) for h in range(2)]
+    EA = [one("es", 4 * h + 3) for h in range(2)]
+    EL = [one("es", 8 + 4 * h + 3) for h in range(2)]
+    NE = [one("par", 4 * h + 2) for h in range(2)]
+
+    hs = helpers(core, nxt, T, topo)
+    hp = helpers(prv, core, T, topo)
+    arrives = sum(len(topo.engines(c, core)) for c in hp) if hp else len(topo.engines(prv, core))
+    sent = [0]
+
+    def send(t):
+        qa, sa, arr = "qa%d" % t, "sa%d" % t, T.sem["arr%d" % t]
+        await_writes("g", W(qa, 0, 32))
+        await_writes("g", W(sa, 0, 128))
+        to = hs if hs else [nxt, nxt]
+        eng = topo.engines(core, to[0])
+        parts = [eng[:len(eng) // 2], eng[len(eng) // 2:]]
+        sides = [(T[qa][:, 0:32].bitcast(dt.uint8), T[qa][:, 128:160].bitcast(dt.uint8)),
+                 (T[sa][:, 0:128], T[sa][:, 128:256])]
+        trs = []
+        for c, e, (a, b) in zip(to, parts, sides):
+            rid, pid = topo.addr(c, core)
+            trs.append(RemoteDMATransfer(dst_ids=[DstId(rid=rid, pnc=pid)], dma_engine_mask=bits(e), remote_sem=arr,
+                                         src=a, dst=b))
+        g.remote_dma_fused(trs, local_sem=T.sem.sent)
+        sent[0] += len(eng)
+
+    moved("s", W("cex"), (W("x16", 32, 48), W("offq")))
+    first_ends()
+    end_gaps(0)
+    quant(W("qu"), W("su"), W("ub"))
+    issue("v", lambda: g.vector.tensor_copy(T.qur[:, 0:128].bitcast(dt.uint32),
+                                            T.qu[:, 0:128].bitcast(dt.uint32).indirect(T.offu[:, 0:8])),
+          [W("qu"), W("offu")], [W("qur")])
+    moved("s", W("sur"), (W("su"), W("offu")))
+    tt(W("dp"), W("de", 0, 32), W("de", 32, 64), alu.mult)
+    stack_masks()
+    order_x("s", 0, 1)
+    order_x("v", 0, 0)
+    quant_x(0, 176)
+    mm(0, 176, W("qur"), W("sur"), W("qx", 0, 176), W("sx", 0, 176))
+    order_x("s", 1, 1)
+    order_x("v", 1, 0)
+    await_writes("y", W("xin"))
+    load("y", W("qw"), T.wc[:], codes=True)
+    load("y", W("sw"), T.ws[:])
+    load("y", W("vb"), T.v[:])
+    quant_x(176, C)
+    mm(1, 176, W("qur"), W("sur"), W("qx", 176, C), W("sx", 176, C))
+    for k in range(3):
+        plane(k)
+    hide(0, 0, 176)
+    own(0, 176)
+    hide(1, 176, C)
+    own(176, C)
+
+    for t in range(ROUNDS):
+        qa, sa = "qa%d" % t, "sa%d" % t
+        last = t == ROUNDS - 1
+        eu = W("eu", 8 * t, 8 * t + 8)
+        scan(W("mm"), W("r22"), W("sc", 15, C, 16), 0.0, alu.max, alu.min)
+        for h in range(2):
+            ts(W("gt", 12 * h + 1, 12 * h + 12), W("mm", 11 * h, 11 * h + 11), one("mm", 11 * h + 10), alu.is_gt)
+        for h in range(2):
+            reduce(K1[h], W("gt", 12 * h, 12 * h + 12), alu.add)
+        for h in range(2):
+            ts(W("offa", h, 8, 2), W("ca", 4 * h, 4 * h + 4), K1[h], alu.add, 64.0, alu.mult)
+        tt(W("s3"), (W("sc"), W("off3")), W("m3"), alu.add)
+        for k in (2, 0, 3, 1):
+            moved("v" if k < 2 else "s", W("xb", XA + k, XA + 128, 4), (XW, W("offa", 2 * k, 2 * k + 2)))
+        scan(W("ls"), W("rst", 0, 96), W("s3"), 0.0, alu.max, alu.min)
+        quant(W(qa, 0, 128), W(sa, 0, 128), W("xb", XA, XA + 512))
+        send(t)
+        plane(3)
+        for h in range(2):
+            ts(W("ind", 4 * h + 1, 4 * h + 3), W("eu", 8 * t + 4 * h, 8 * t + 4 * h + 2), K1[h], alu.is_lt)
+        if t == 0:
+            iota(W("tab"), [[1, PL]], 1)
+            issue("g", lambda: g.affine_select(T.et[:], T.c64[:], [[-1, 516]], alu.is_equal, 0.0, 3, 4), [W("c64")], [W("et")])
+        for h in range(2):
+            low = W("ls", 15 + 16 * h, 96, 32)
+            scan(W("pm", 4 * h, 4 * h + 3), low, low, -TOP, alu.max, alu.max)
+        tt(W("pr", 0, 8), W("ind", 0, 8), eu, alu.mult)
+        for h in range(2):
+            ts(W("ind", 8 + 4 * h + 1, 8 + 4 * h + 3), W("pm", 4 * h, 4 * h + 2), one("pm", 4 * h + 2), alu.is_lt)
+        ts(pair("par", 2), pair("pm", 2), TOP, alu.is_lt, 16.0, alu.mult)
+        tt(pair("ind", 9), pair("ind", 9), pair("ind", 1), alu.is_ge)
+        filler()
+        tt(W("pr", 8, 16), W("ind", 8, 16), eu, alu.mult)
+        tt(W("dl"), W("ind", 0, 8), W("ind", 8, 16), alu.subtract)
+        scan(W("es"), W("c4"), W("pr"), 0.0, alu.mult, alu.max)
+        filler()
+        tt(pair("par", 0), pair("es", 3), pair("cof", 1), alu.subtract)
+        tt(pair("par", 3), pair("es", 11), pair("es", 3), alu.is_ge)
+        moved("s", pair("cof", 2), pair("es", 3))
+        for h in range(2):
+            activ(one("vc", h), EL[h], act.Identity, NE[h])
+        for h in range(2):
+            activ(W("vv", 11 * h, 11 * h + 11), W("kn"), act.Identity, NE[h], one("vc", h))
+        ts(W("cl", 0, 11), W("kp", 0, 11), K1[0], alu.max, EA[0], alu.min)
+        tt(pair("par", 1), pair("par", 0), pair("par", 3), alu.mult)
+        ts(W("cl", 11, 22), W("kp", 0, 11), K1[1], alu.max, EA[1], alu.min)
+        tt(pair("stp", 2), pair("es", 11), pair("par", 1), alu.subtract)
+        tt(pair("stp", 1), pair("es", 3), pair("par", 1), alu.subtract)
+        tt(pair("stp", 0), pair("stp", 2), pair("par", 0), alu.add)
+        tt(pair("cof", 3), pair("stp", 1), pair("stp", 2), alu.add)
+        for h in range(2):
+            for e in range(2):
+                j = 4 * h + e
+                activ(one("eu", 8 * t + 8 + j), one("dl", j + 1), act.Identity, NN[h], one("eu", 8 * t + j))
+        if not last:
+            end_gaps(t + 1)
+        tt(W("st1"), (W("stp"), W("offs")), W("ys"), alu.is_le)
+        tt(pair("cof", 0), pair("cof", 3), pair("par", 0), alu.add)
+        tt(W("eq"), W("cl"), W("kp"), alu.is_equal)
+        filler(2)
+        tt(W("st2"), (W("cof"), W("offc")), W("cofc"), alu.add)
+        tt(W("wm"), W("eq"), W("vv"), alu.mult)
+        filler()
+        tt(W("st3"), W("st1"), W("st2"), alu.mult)
+        tt(W("mf"), W("wm"), W("bm"), alu.add)
+        filler()
+        scan(W("st4"), W("ch"), W("st3"), 0.0, alu.mult, alu.add)
+        copy(W("offm"), W("mf"))
+        filler()
+        tt(W("ef"), W("st4", 3, 96, 4), W("yb"), alu.add)
+        filler()
+        ts(W("offe"), W("ef"), 16.0, alu.mult)
+        moved("s", W("i1"), (W("tab"), W("offe")))
+        moved("s", W("i2"), (W("i1"), W("offd")))
+        if not last:
+            moved("s", W("i3"), (W("i2"), W("offn")))
+        both(0)
+        if not last:
+            tt(W("dp"), W("de", 0, 32), W("de", 32, 64), alu.mult)
+        if last:
+            e3 = 8 * ROUNDS
+            iota(W("ho"), [[0, 32]])
+            moved("s", W("ho", 0, 2), pair("eu", e3))
+            tt(W("ho", 2, 4), pair("eu", e3 + 1), pair("eu", e3), alu.subtract)
+            tt(W("ho", 4, 6), pair("eu", e3 + 2), pair("eu", e3 + 1), alu.subtract)
+        both(1)
+        both(2)
+        if t == 0:
+            for b in range(4):
+                quant(W("qe", 128 * b, 128 * b + 128), W("se", 128 * b, 128 * b + 128), W("et", 3 - b, 515 - b))
+        if last:
+            issue("v", lambda: g.vector.transpose(T.ht[:], T.ho[:]), [W("ho")], [W("ht")])
+            for gg in range(8):
+                a, e = gg // 2, gg % 2
+                store("y", T.oh[gg:gg + 1, :], W("ht", 16 * e, 16 * e + 16, 1, 32 * a, 32 * a + 6))
+        both(3)
+        g.tensor.wait_ge(T.sem["arr%d" % t], arrives)
+        for b in range(4):
+            mm(b, 128, W("qe", 128 * b, 128 * b + 128), W("se", 128 * b, 128 * b + 128), W(qa, 32, 160), W(sa, 32, 160))
+        for b in range(4):
+            mm(4 + b, 128, W("qe", 128 * b, 128 * b + 128), W("se", 128 * b, 128 * b + 128), W(qa, 32, 160), W(sa, 32, 160),
+               True, False)
+        for b in range(4):
+            scaled("s", W("xb", XG + b, XG + 128, 4), W("ps", 512 * b + 96, 512 * b + 128), 1.0 / 64)
+        quant(W("qg"), W("sg"), W("xb", XG - 384, XG + 128))
+        if not last:
+            stack_masks()
+        for b in range(4):
+            mm(4 + b, 128, W("qw", 128 * b, 128 * b + 128), W("sw", 128 * b, 128 * b + 128), W("qg"), W("sg"), False, True)
+        scan(W("ex"), W("cex"), W("i2" if last else "i3"), 0.0, alu.mult, alu.max)
+        for b in range(4):
+            scaled("s", W("zz", PL * b + C, PL * b + PL), W("ps", 512 * (4 + b) + 96, 512 * (4 + b) + 128), 1.0 / 32)
+        ts(W("offf"), W("ex", 15, C, 16), INV, alu.mult, -1.0, alu.add)
+        if t == 1:
+            quant(W("qv"), W("sv"), W("vb"))
+        cut = 14 if last else 12
+        c1 = 16 * cut
+        st = (W("qv"), W("sv")) if last else (W("qur"), W("sur"))
+        deal("v", 0, 0, cut)
+        deal("v", 1, 0, cut)
+        deal("s", 3, 0, cut)
+        deal("v", 2, 0, cut)
+        deal("s", 0, cut, 22)
+        quant_x(0, c1)
+        mm(0, c1, st[0], st[1], W("qx", 0, c1), W("sx", 0, c1))
+        deal("s", 1, cut, 22)
+        deal("v", 3, cut, 22)
+        deal("s", 2, cut, 22)
+        if not last:
+            hide(0, 0, c1)
+            quant_x(c1, C)
+            mm(1, C - c1, st[0], st[1], W("qx", c1, C), W("sx", c1, C))
+            for k in range(3):
+                plane(k)
+            own(0, c1)
+            hide(1, c1, C)
+            own(c1, C)
+        else:
+            store("y", T.oc[:, 0:4 * c1], W("qx", 0, c1), codes=True)
+            quant_x(c1, C)
+            mm(1, C - c1, st[0], st[1], W("qx", c1, C), W("sx", c1, C))
+            moved("s", W("ysb", 0, c1), W("ps", 0, c1))
+            store("y", T.oc[:, 4 * c1:4 * C], W("qx", c1, C), codes=True)
+            store("s", T.y[:, 0:c1], W("ysb", 0, c1))
+            for k in range(4):
+                store("y" if k < 2 else "s", T.osc[4 * k:4 * k + 4, :], W("sx", 0, C, 1, 32 * k, 32 * k + 4))
+            copy(W("ysb", c1, C), W("ps", 512, 512 + C - c1))
+            store("y", T.y[:, c1:C], W("ysb", c1, C))
+
+    g.wait_ge(T.sem.sent, sent[0])
+    for q in ENGSEM:
+        learn("y", ENGSEM[q], count[q], {})
+    for i in range(dmas[0]):
+        learn("y", "dma%d" % i, 16, {})

@@ -5,46 +5,25 @@ C, V, B, ROUNDS = 352, 11, 32, 3
 XA, XX, XG = 0, 128, 128 + 4 * C
 PL = C + B
 BIG, TOP = 2.0 ** 90, 2.0 ** 80
-
 F32, BF, I32, U16, CODE, PLANE = "float32", "bfloat16", "int32", "uint16", "float8_e4m3fn_x4", "uint8"
+SCRATCH = {"ps": ("psum", [128, 4096], F32)}
+for _d, _l in (
+    (BF, dict(xin=4 * C, xb=XG + 128, zz=4 * PL, xp=4 * C, ub=512, vb=512, et=516, c64=516)),
+    (CODE, dict(qu=128, qur=128, qv=128, qw=512, qe=512, qx=C, qg=128, qa0=160, qa1=160, qa2=160)),
+    (PLANE, dict(su=128, sur=128, sv=128, sw=512, se=512, sx=C, sg=128, sa0=256, sa1=256, sa2=256)),
+    (I32, dict(hgi=6, dgi=22, pi=2, pj=2, ti=22, fi=2)),
+    (F32, dict(col=16, i32=32, i44=44, sm=64, tab=PL, m16=16, r16=16, x16=48, maskq=C, rst=C, cex=C, bb=C, sc=C, r22=22,
+               mm=22, gt=24, ca=8, kp=22, kn=11, k05=16, de=64, dp=32, m3=96, s3=96, ls=96, pm=8, ind=16, eu=32, pr=16,
+               es=16, c4=16, par=8, stp=8, cof=8, dl=8, vc=2, ys=96, cofc=96, ch=96, st1=96, st2=96, st3=96, st4=96,
+               yi=24, yb=24, ef=24, cl=22, vv=22, eq=22, wm=22, mf=22, bi=22, bm=22, d1=22, d2=22, d3=22, d4=22, d5=22,
+               d6=22, i1=PL, i2=C, i3=C, ex=C, hf=8, ho=32, ht=32, ysb=C)),
+    (U16, dict(offp=44, offq=22, offu=8, offn=22, offa=8, off3=6, offs=6, offc=6, offe=24, offd=22, offo=22, offm=22,
+               offf=22)),
+):
+    for _n, _w in _l.items():
+        SCRATCH[_n] = ("sbuf", [128, _w], _d)
 
-
-def _sb(n, d):
-    return ("sbuf", [128, n], d)
-
-
-SCRATCH = {
-    "xin": _sb(4 * C, BF), "xb": _sb(XG + 128, BF), "zz": _sb(4 * PL, BF), "xp": _sb(4 * C, BF),
-    "ub": _sb(512, BF), "vb": _sb(512, BF), "et": _sb(516, BF), "c64": _sb(516, BF),
-    "qu": _sb(128, CODE), "su": _sb(128, PLANE), "qur": _sb(128, CODE), "sur": _sb(128, PLANE),
-    "qv": _sb(128, CODE), "sv": _sb(128, PLANE), "qw": _sb(512, CODE), "sw": _sb(512, PLANE),
-    "qe": _sb(512, CODE), "se": _sb(512, PLANE), "qx": _sb(C, CODE), "sx": _sb(C, PLANE),
-    "qg": _sb(128, CODE), "sg": _sb(128, PLANE),
-    "hgi": _sb(6, I32), "dgi": _sb(22, I32), "pi": _sb(2, I32), "pj": _sb(2, I32), "ti": _sb(22, I32), "fi": _sb(2, I32),
-    "col": _sb(16, F32), "i32": _sb(32, F32), "i44": _sb(44, F32), "sm": _sb(64, F32), "tab": _sb(PL, F32),
-    "m16": _sb(16, F32), "r16": _sb(16, F32), "x16": _sb(48, F32),
-    "maskq": _sb(C, F32), "rst": _sb(C, F32), "cex": _sb(C, F32),
-    "bb": _sb(C, F32), "sc": _sb(C, F32), "r22": _sb(22, F32), "mm": _sb(22, F32), "gt": _sb(24, F32),
-    "ca": _sb(8, F32), "kp": _sb(22, F32), "kn": _sb(11, F32), "k05": _sb(16, F32), "de": _sb(64, F32), "dp": _sb(32, F32),
-    "m3": _sb(96, F32), "s3": _sb(96, F32), "ls": _sb(96, F32), "pm": _sb(8, F32),
-    "ind": _sb(16, F32), "eu": _sb(8 * (ROUNDS + 1), F32), "pr": _sb(16, F32), "es": _sb(16, F32), "c4": _sb(16, F32),
-    "par": _sb(8, F32), "stp": _sb(8, F32), "cof": _sb(8, F32), "dl": _sb(8, F32), "vc": _sb(2, F32),
-    "ys": _sb(96, F32), "cofc": _sb(96, F32), "ch": _sb(96, F32), "st1": _sb(96, F32), "st2": _sb(96, F32),
-    "st3": _sb(96, F32), "st4": _sb(96, F32), "yi": _sb(24, F32), "yb": _sb(24, F32), "ef": _sb(24, F32),
-    "cl": _sb(22, F32), "vv": _sb(22, F32), "eq": _sb(22, F32), "wm": _sb(22, F32), "mf": _sb(22, F32),
-    "bi": _sb(22, F32), "bm": _sb(22, F32),
-    "d1": _sb(22, F32), "d2": _sb(22, F32), "d3": _sb(22, F32), "d4": _sb(22, F32), "d5": _sb(22, F32), "d6": _sb(22, F32),
-    "i1": _sb(PL, F32), "i2": _sb(C, F32), "i3": _sb(C, F32), "ex": _sb(C, F32),
-    "hf": _sb(8, F32), "ho": _sb(32, F32), "ht": _sb(32, F32), "ysb": _sb(C, F32),
-    "offp": _sb(44, U16), "offq": _sb(22, U16), "offu": _sb(8, U16), "offn": _sb(22, U16), "offa": _sb(8, U16),
-    "off3": _sb(6, U16), "offs": _sb(6, U16), "offc": _sb(6, U16), "offe": _sb(24, U16),
-    "offd": _sb(22, U16), "offm": _sb(22, U16), "offf": _sb(22, U16),
-    "ps": ("psum", [128, 4096], F32),
-}
-for _t in range(ROUNDS):
-    SCRATCH["qa%d" % _t] = _sb(160, CODE)
-    SCRATCH["sa%d" % _t] = _sb(256, PLANE)
-
+WAKE, FAR, ISSUE, SLACK = 150, 4000, 60, 60
 NDMA = 26
 ENGSEM = {"v": "cv", "s": "cs", "p": "cp", "g": "cg"}
 SEMAPHORES = ["cv", "cs", "cp", "cg", "sent"] + ["arr%d" % t for t in range(ROUNDS)] + ["dma%d" % i for i in range(NDMA)]
@@ -115,58 +94,134 @@ def rank_program(g, core, T, topo):
         return m
 
     touched = {}
-    known = {q: {} for q in queue}
-    count = {q: 0 for q in ENGSEM}
-    dmas = [0]
+    ops = []
+    loads = {q: [] for q in queue}
 
-    def learn(q, sem, val, clock):
-        if known[q].get(sem, 0) >= val:
-            return
-        queue[q].wait_ge(T.sem[sem], val)
-        known[q][sem] = val
-        for s2, v2 in clock.items():
-            if known[q].get(s2, 0) < v2:
-                known[q][s2] = v2
+    def width(v):
+        return 16 * (v[1][2] - v[1][1]) if len(v) == 2 else len(range(v[1], v[2], v[3]))
 
-    def issue(q, call, reads, writes, dma=False, chained=False):
-        need = []
+    def issue(q, call, reads, writes, cost, dma=False, chained=False, far=None):
+        need, order = set(), set()
         for views, wr in ((reads, False), (writes, True)):
             for v in views:
                 m = cover(v)
-                for (m2, wr2, q2, sem, val, clock) in touched.get(v[0], []):
+                for (m2, wr2, j) in touched.get(v[0], []):
                     if not m & m2:
                         continue
                     if v[0] == "ps":
-                        if q2 == q and (chained or not (wr or wr2)):
+                        if ops[j]["q"] == q and (chained or not (wr or wr2)):
+                            order.add(j)
                             continue
                     elif not (wr or wr2):
                         continue
-                    need.append((sem, val, clock))
-        need.sort(key=lambda e: -e[1])
-        for sem, val, clock in need:
-            learn(q, sem, val, clock)
-        ins = call()
-        if dma:
-            sem, val = "dma%d" % dmas[0], 16
-            dmas[0] += 1
-            ins.then_inc(T.sem[sem], 16)
-        else:
-            count[q] += 1
-            sem, val = ENGSEM[q], count[q]
-            ins.then_inc(T.sem[sem], 1)
-        clock = dict(known[q])
+                    need.add(j)
+        if dma and not reads:
+            order.update(loads[q][-1:])
+            loads[q].append(len(ops))
+        ops.append(dict(q=q, call=call, need=need, order=order - need, cost=cost, dma=dma, far=far))
         for views, wr in ((reads, False), (writes, True)):
             for v in views:
                 m = cover(v)
                 old = touched.setdefault(v[0], [])
                 if wr:
                     old[:] = [e for e in old if e[0] & ~m]
-                old.append((m, wr, q, sem, val, clock))
+                old.append((m, wr, len(ops) - 1))
 
-    def await_writes(q, v):
-        for (m2, wr2, q2, sem, val, clock) in touched[v[0]]:
-            if wr2 and m2 & cover(v):
+    def plan():
+        late = [o["cost"] for o in ops]
+        rest = [0.0] * len(ops)
+        before = []
+        for i, o in enumerate(ops):
+            e = [(j, WAKE) for j in o["need"]] + [(j, ISSUE - late[j] if o["dma"] else 0) for j in o["order"]]
+            if o["far"] is not None:
+                e.append((sends[o["far"]], FAR))
+            before.append(e)
+        for i in range(len(ops) - 1, -1, -1):
+            rest[i] += late[i]
+            for j, w in before[i]:
+                rest[j] = max(rest[j], rest[i] + w)
+        after = [[] for _ in ops]
+        left = [len(e) for e in before]
+        for i, e in enumerate(before):
+            for j, w in e:
+                after[j].append(i)
+        ready = {q: [] for q in queue}
+        for i, o in enumerate(ops):
+            if not left[i]:
+                ready[o["q"]].append(i)
+        free = {q: 0.0 for q in queue}
+        end = [0.0] * len(ops)
+        seq = []
+
+        def start(i):
+            return max([free[ops[i]["q"]]] + [end[j] + w for j, w in before[i]])
+
+        while len(seq) < len(ops):
+            pick = None
+            for q in queue:
+                if not ready[q]:
+                    continue
+                top = max(ready[q], key=lambda i: (rest[i], -i))
+                s = start(top)
+                fit = [i for i in ready[q] if start(i) < s and start(i) + (ISSUE if ops[i]["dma"] else late[i]) <= s + SLACK]
+                if fit:
+                    top = min(fit, key=lambda i: (start(i), -rest[i], i))
+                if pick is None or start(top) < start(pick):
+                    pick = top
+            s, o = start(pick), ops[pick]
+            end[pick] = s + late[pick]
+            free[o["q"]] = s + ISSUE if o["dma"] else end[pick]
+            ready[o["q"]].remove(pick)
+            seq.append(pick)
+            for i in after[pick]:
+                left[i] -= 1
+                if not left[i]:
+                    ready[ops[i]["q"]].append(i)
+        return seq
+
+    def emit(seq):
+        known = {q: {} for q in queue}
+        count = {q: 0 for q in ENGSEM}
+        mark, dmas = {}, 0
+
+        def learn(q, sem, val, clock):
+            if known[q].get(sem, 0) >= val:
+                return
+            queue[q].wait_ge(T.sem[sem], val)
+            known[q][sem] = val
+            for s2, v2 in clock.items():
+                if known[q].get(s2, 0) < v2:
+                    known[q][s2] = v2
+
+        for i in seq:
+            o = ops[i]
+            q = o["q"]
+            for sem, val, clock in sorted((mark[j] for j in o["need"]), key=lambda e: -e[1]):
                 learn(q, sem, val, clock)
+            if o["far"] is not None:
+                learn(q, "arr%d" % o["far"], arrives, {})
+            ins = o["call"]()
+            if ins is None:
+                continue
+            if o["dma"]:
+                sem, val = "dma%d" % dmas, 16
+                dmas += 1
+                ins.then_inc(T.sem[sem], 16)
+            else:
+                count[q] += 1
+                sem, val = ENGSEM[q], count[q]
+                ins.then_inc(T.sem[sem], 1)
+            mark[i] = (sem, val, dict(known[q]))
+        g.wait_ge(T.sem.sent, ROUNDS * len(topo.engines(core, hs[0] if hs else nxt)))
+        for q in ENGSEM:
+            learn("y", ENGSEM[q], count[q], {})
+        for i in range(dmas):
+            learn("y", "dma%d" % i, 16, {})
+
+    def took(q, i, per=1.0):
+        if len(i) == 2:
+            return (50 if q == "v" else 65) + 1.3 * width(i)
+        return max(64, width(i) * per) + (0 if q == "v" else 60)
 
     def src(v):
         if len(v) == 2:
@@ -177,39 +232,40 @@ def rank_program(g, core, T, topo):
         return (ap(s), [s]) if isinstance(s, tuple) else (s, [])
 
     def memset(o, c):
-        issue("v", lambda: g.vector.memset(ap(o), c), [], [o])
+        issue("v", lambda: g.vector.memset(ap(o), c), [], [o], took("v", o, 0.5))
 
     def copy(o, i):
         a, r = src(i)
-        issue("v", lambda: g.vector.tensor_copy(ap(o), a), r, [o])
+        issue("v", lambda: g.vector.tensor_copy(ap(o), a), r, [o], took("v", i))
 
     def tt(o, i0, i1, op):
         a, r = src(i0)
-        issue("v", lambda: g.vector.tensor_tensor(ap(o), a, ap(i1), op), r + [i1], [o])
+        issue("v", lambda: g.vector.tensor_tensor(ap(o), a, ap(i1), op), r + [i1], [o],
+              took("v", i0, 1.0 if i0[0] == "ps" else 2.0))
 
     def ts(o, i0, s1, op0, s2=None, op1=None):
         a, r = src(i0)
         x1, r1 = scal(s1)
         x2, r2 = scal(s2)
         if op1 is None:
-            issue("v", lambda: g.vector.tensor_scalar(ap(o), a, x1, None, op0), r + r1, [o])
+            issue("v", lambda: g.vector.tensor_scalar(ap(o), a, x1, None, op0), r + r1, [o], took("v", i0))
         else:
-            issue("v", lambda: g.vector.tensor_scalar(ap(o), a, x1, x2, op0, op1), r + r1 + r2, [o])
+            issue("v", lambda: g.vector.tensor_scalar(ap(o), a, x1, x2, op0, op1), r + r1 + r2, [o], took("v", i0))
 
     def scan(o, d0, d1, init, op0, op1):
-        issue("v", lambda: g.vector.tensor_tensor_scan(ap(o), ap(d0), ap(d1), init, op0, op1), [d0, d1], [o])
+        issue("v", lambda: g.vector.tensor_tensor_scan(ap(o), ap(d0), ap(d1), init, op0, op1), [d0, d1], [o], took("v", d0))
 
     def reduce(o, i, op):
-        issue("v", lambda: g.vector.tensor_reduce(ap(o), ap(i), AxisListType.X, op), [i], [o])
+        issue("v", lambda: g.vector.tensor_reduce(ap(o), ap(i), AxisListType.X, op), [i], [o], took("v", i))
 
     def quant(q, s, i):
-        issue("v", lambda: g.vector.quantize_mx(ap(q), ap(s), ap(i)), [i], [q, s])
+        issue("v", lambda: g.vector.quantize_mx(ap(q), ap(s), ap(i)), [i], [q, s], 12 + 0.22 * width(i))
 
     def activ(o, i, func, scale=1.0, bias=0.0):
         a, r = src(i)
         x, r1 = scal(scale)
         y, r2 = scal(bias)
-        issue("s", lambda: g.scalar.activation(ap(o), a, func, bias=y, scale=x), r + r1 + r2, [o])
+        issue("s", lambda: g.scalar.activation(ap(o), a, func, bias=y, scale=x), r + r1 + r2, [o], took("s", i))
 
     def scaled(q, o, i, c):
         if q == "v":
@@ -222,26 +278,27 @@ def rank_program(g, core, T, topo):
             copy(o, i)
         else:
             a, r = src(i)
-            issue("s", lambda: g.scalar.activation(ap(o), a, act.Copy), r, [o])
+            issue("s", lambda: g.scalar.activation(ap(o), a, act.Copy), r, [o], took("s", i))
 
-    def mm(bank, ncol, wq, ws, xq, xs, start=True, stop=True):
+    def mm(bank, ncol, wq, ws, xq, xs, start=True, stop=True, far=None):
         o = W("ps", 512 * bank, 512 * bank + ncol)
         issue("p", lambda: g.tensor.matmul_mx(ap(o), ap(wq), ap(ws), ap(xq), ap(xs), start, stop),
-              [wq, ws, xq, xs], [o], chained=not start)
+              [wq, ws, xq, xs], [o], ncol + 16, chained=not start, far=far)
 
     def iota(o, pattern, base=0, cm=0):
         if SCRATCH[o[0]][2] == I32:
-            issue("g", lambda: g.iota(ap(o), pattern, base, cm), [], [o])
+            issue("g", lambda: g.iota(ap(o), pattern, base, cm), [], [o], 130 + 2 * width(o))
         else:
-            issue("g", lambda: g.iota(ap(o), pattern, base, cm, allow_small_or_imprecise_dtypes=True), [], [o])
+            issue("g", lambda: g.iota(ap(o), pattern, base, cm, allow_small_or_imprecise_dtypes=True), [], [o],
+                  130 + 2 * width(o))
 
-    def load(q, o, i, codes=False):
+    def load(q, o, i, cost, codes=False, behind=()):
         a = ap(o).bitcast(dt.uint8) if codes else ap(o)
-        issue(q, lambda: queue[q].dma_start(a, i), [], [o], dma=True)
+        issue(q, lambda: queue[q].dma_start(a, i), list(behind), [o], cost, dma=True)
 
     def store(q, o, i, codes=False):
         a = ap(i).bitcast(dt.uint8) if codes else ap(i)
-        issue(q, lambda: queue[q].dma_start(o, a), [i], [], dma=True)
+        issue(q, lambda: queue[q].dma_start(o, a), [i], [], 2500, dma=True)
 
     def one(name, j):
         return W(name, j, j + 1)
@@ -250,11 +307,11 @@ def rank_program(g, core, T, topo):
         return W(name, j, j + 5, 4)
 
     half = 2 * C
-    load("y", W("ub"), T.u[:])
-    load("s", W("hgi"), T.hg[:])
-    load("y", W("xin", 0, half), T.x[:, 0:half])
-    load("s", W("dgi"), T.dg[:])
-    load("y", W("xin", half, 2 * half), T.x[:, half:2 * half])
+    load("y", W("ub"), T.u[:], 2500)
+    load("s", W("hgi"), T.hg[:], 2200)
+    load("y", W("xin", 0, half), T.x[:, 0:half], 3100)
+    load("s", W("dgi"), T.dg[:], 2200)
+    load("y", W("xin", half, 2 * half), T.x[:, half:2 * half], 3700)
 
     Q, Q3, Q11, PP, Q4, QC, INV, FS = [one("col", j) for j in range(8)]
     iota(W("pi"), [[0, 2]], 0, 1)
@@ -266,8 +323,8 @@ def rank_program(g, core, T, topo):
     iota(W("sm", 24, 46), [[176, 2], [1, 11]])
     iota(W("yi"), [[176, 2], [16, 12]])
     iota(W("bi"), [[16, 22]])
-    iota(W("eu"), [[0, 8 * (ROUNDS + 1)]])
-    iota(W("eu", 2, 8 * (ROUNDS + 1), 4), [[0, 2 * (ROUNDS + 1)]], V)
+    iota(W("eu"), [[0, 32]])
+    iota(W("eu", 2, 32, 4), [[0, 8]], V)
     iota(W("gt"), [[0, 24]], 1)
     iota(W("kp"), [[0, 2], [1, 11]], 1)
     iota(W("kn"), [[-1, 11]], -1)
@@ -319,27 +376,6 @@ def rank_program(g, core, T, topo):
     ts(W("yb"), W("yi"), Q, alu.add, 1.0 / 16, alu.mult)
     ts(W("bm"), W("bi"), Q, alu.add)
 
-    dealing = [
-        lambda: ts(W("d2"), W("dgi"), -5.0, alu.add, 1.0 / V, alu.mult),
-        lambda: copy(W("ti"), W("d2")),
-        lambda: ts(W("d1"), W("dgi"), 16.0, alu.mult),
-        lambda: ts(W("d3"), W("ti"), -175.0, alu.mult),
-        lambda: ts(W("d4"), W("ti"), 16.0, alu.is_ge, 176.0, alu.mult),
-        lambda: tt(W("d5"), W("d1"), W("d3"), alu.add),
-        lambda: tt(W("d6"), W("d5"), W("d4"), alu.add),
-        lambda: copy(W("offd"), W("d6")),
-    ]
-
-    def filler(k=1):
-        for _ in range(k):
-            if dealing:
-                dealing.pop(0)()
-
-    def first_ends():
-        copy(W("hf", 0, 6), W("hgi"))
-        copy(pair("eu", 0), W("hf", 0, 2))
-        tt(pair("eu", 1), W("hf", 0, 2), W("hf", 2, 4), alu.add)
-
     def end_gaps(t):
         for e in range(2):
             for h in range(2):
@@ -384,12 +420,10 @@ def rank_program(g, core, T, topo):
     hs = helpers(core, nxt, T, topo)
     hp = helpers(prv, core, T, topo)
     arrives = sum(len(topo.engines(c, core)) for c in hp) if hp else len(topo.engines(prv, core))
-    sent = [0]
+    sends = []
 
     def send(t):
         qa, sa, arr = "qa%d" % t, "sa%d" % t, T.sem["arr%d" % t]
-        await_writes("g", W(qa, 0, 32))
-        await_writes("g", W(sa, 0, 128))
         to = hs if hs else [nxt, nxt]
         eng = topo.engines(core, to[0])
         parts = [eng[:len(eng) // 2], eng[len(eng) // 2:]]
@@ -400,16 +434,35 @@ def rank_program(g, core, T, topo):
             rid, pid = topo.addr(c, core)
             trs.append(RemoteDMATransfer(dst_ids=[DstId(rid=rid, pnc=pid)], dma_engine_mask=bits(e), remote_sem=arr,
                                          src=a, dst=b))
-        g.remote_dma_fused(trs, local_sem=T.sem.sent)
-        sent[0] += len(eng)
+
+        def call():
+            g.remote_dma_fused(trs, local_sem=T.sem.sent)
+
+        sends.append(len(ops))
+        issue("g", call, [W(qa, 0, 32), W(sa, 0, 128)], [], 300)
 
     moved("s", W("cex"), (W("x16", 32, 48), W("offq")))
-    first_ends()
+    iota(W("tab"), [[1, PL]], 1)
+    ts(W("d2"), W("dgi"), -5.0, alu.add, 1.0 / V, alu.mult)
+    copy(W("ti"), W("d2"))
+    ts(W("d1"), W("dgi"), 16.0, alu.mult)
+    ts(W("d3"), W("ti"), -175.0, alu.mult)
+    ts(W("d4"), W("ti"), 16.0, alu.is_ge, 176.0, alu.mult)
+    tt(W("d5"), W("d1"), W("d3"), alu.add)
+    tt(W("d6"), W("d5"), W("d4"), alu.add)
+    copy(W("offd"), W("d6"))
+    moved("s", W("i2"), (W("tab"), W("offd")))
+    moved("s", W("i3"), (W("i2"), W("offn")))
+    scan(W("ex"), W("cex"), W("i3"), 0.0, alu.mult, alu.max)
+    ts(W("offo"), W("ex", 15, C, 16), INV, alu.mult, -1.0, alu.add)
+    copy(W("hf", 0, 6), W("hgi"))
+    copy(pair("eu", 0), W("hf", 0, 2))
+    tt(pair("eu", 1), W("hf", 0, 2), W("hf", 2, 4), alu.add)
     end_gaps(0)
     quant(W("qu"), W("su"), W("ub"))
     issue("v", lambda: g.vector.tensor_copy(T.qur[:, 0:128].bitcast(dt.uint32),
                                             T.qu[:, 0:128].bitcast(dt.uint32).indirect(T.offu[:, 0:8])),
-          [W("qu"), W("offu")], [W("qur")])
+          [W("qu"), W("offu")], [W("qur")], 220)
     moved("s", W("sur"), (W("su"), W("offu")))
     tt(W("dp"), W("de", 0, 32), W("de", 32, 64), alu.mult)
     stack_masks()
@@ -419,10 +472,9 @@ def rank_program(g, core, T, topo):
     mm(0, 176, W("qur"), W("sur"), W("qx", 0, 176), W("sx", 0, 176))
     order_x("s", 1, 1)
     order_x("v", 1, 0)
-    await_writes("y", W("xin"))
-    load("y", W("qw"), T.wc[:], codes=True)
-    load("y", W("sw"), T.ws[:])
-    load("y", W("vb"), T.v[:])
+    load("y", W("qw"), T.wc[:], 3000, codes=True, behind=[W("xin")])
+    load("y", W("sw"), T.ws[:], 3200, behind=[W("xin")])
+    load("y", W("vb"), T.v[:], 3600, behind=[W("xin")])
     quant_x(176, C)
     mm(1, 176, W("qur"), W("sur"), W("qx", 176, C), W("sx", 176, C))
     for k in range(3):
@@ -453,8 +505,8 @@ def rank_program(g, core, T, topo):
         for h in range(2):
             ts(W("ind", 4 * h + 1, 4 * h + 3), W("eu", 8 * t + 4 * h, 8 * t + 4 * h + 2), K1[h], alu.is_lt)
         if t == 0:
-            iota(W("tab"), [[1, PL]], 1)
-            issue("g", lambda: g.affine_select(T.et[:], T.c64[:], [[-1, 516]], alu.is_equal, 0.0, 3, 4), [W("c64")], [W("et")])
+            issue("g", lambda: g.affine_select(T.et[:], T.c64[:], [[-1, 516]], alu.is_equal, 0.0, 3, 4), [W("c64")],
+                  [W("et")], 1200)
         for h in range(2):
             low = W("ls", 15 + 16 * h, 96, 32)
             scan(W("pm", 4 * h, 4 * h + 3), low, low, -TOP, alu.max, alu.max)
@@ -463,11 +515,9 @@ def rank_program(g, core, T, topo):
             ts(W("ind", 8 + 4 * h + 1, 8 + 4 * h + 3), W("pm", 4 * h, 4 * h + 2), one("pm", 4 * h + 2), alu.is_lt)
         ts(pair("par", 2), pair("pm", 2), TOP, alu.is_lt, 16.0, alu.mult)
         tt(pair("ind", 9), pair("ind", 9), pair("ind", 1), alu.is_ge)
-        filler()
         tt(W("pr", 8, 16), W("ind", 8, 16), eu, alu.mult)
         tt(W("dl"), W("ind", 0, 8), W("ind", 8, 16), alu.subtract)
         scan(W("es"), W("c4"), W("pr"), 0.0, alu.mult, alu.max)
-        filler()
         tt(pair("par", 0), pair("es", 3), pair("cof", 1), alu.subtract)
         tt(pair("par", 3), pair("es", 11), pair("es", 3), alu.is_ge)
         moved("s", pair("cof", 2), pair("es", 3))
@@ -491,23 +541,16 @@ def rank_program(g, core, T, topo):
         tt(W("st1"), (W("stp"), W("offs")), W("ys"), alu.is_le)
         tt(pair("cof", 0), pair("cof", 3), pair("par", 0), alu.add)
         tt(W("eq"), W("cl"), W("kp"), alu.is_equal)
-        filler(2)
         tt(W("st2"), (W("cof"), W("offc")), W("cofc"), alu.add)
         tt(W("wm"), W("eq"), W("vv"), alu.mult)
-        filler()
         tt(W("st3"), W("st1"), W("st2"), alu.mult)
         tt(W("mf"), W("wm"), W("bm"), alu.add)
-        filler()
         scan(W("st4"), W("ch"), W("st3"), 0.0, alu.mult, alu.add)
         copy(W("offm"), W("mf"))
-        filler()
         tt(W("ef"), W("st4", 3, 96, 4), W("yb"), alu.add)
-        filler()
         ts(W("offe"), W("ef"), 16.0, alu.mult)
         moved("s", W("i1"), (W("tab"), W("offe")))
-        moved("s", W("i2"), (W("i1"), W("offd")))
-        if not last:
-            moved("s", W("i3"), (W("i2"), W("offn")))
+        moved("s", W("i2"), (W("i1"), W("offd" if last else "offo")))
         both(0)
         if not last:
             tt(W("dp"), W("de", 0, 32), W("de", 32, 64), alu.mult)
@@ -523,17 +566,16 @@ def rank_program(g, core, T, topo):
             for b in range(4):
                 quant(W("qe", 128 * b, 128 * b + 128), W("se", 128 * b, 128 * b + 128), W("et", 3 - b, 515 - b))
         if last:
-            issue("v", lambda: g.vector.transpose(T.ht[:], T.ho[:]), [W("ho")], [W("ht")])
+            issue("v", lambda: g.vector.transpose(T.ht[:], T.ho[:]), [W("ho")], [W("ht")], 64)
             for gg in range(8):
                 a, e = gg // 2, gg % 2
                 store("y", T.oh[gg:gg + 1, :], W("ht", 16 * e, 16 * e + 16, 1, 32 * a, 32 * a + 6))
         both(3)
-        g.tensor.wait_ge(T.sem["arr%d" % t], arrives)
         for b in range(4):
-            mm(b, 128, W("qe", 128 * b, 128 * b + 128), W("se", 128 * b, 128 * b + 128), W(qa, 32, 160), W(sa, 32, 160))
+            mm(b, 128, W("qe", 128 * b, 128 * b + 128), W("se", 128 * b, 128 * b + 128), W(qa, 32, 160), W(sa, 32, 160), far=t)
         for b in range(4):
             mm(4 + b, 128, W("qe", 128 * b, 128 * b + 128), W("se", 128 * b, 128 * b + 128), W(qa, 32, 160), W(sa, 32, 160),
-               True, False)
+               True, False, far=t)
         for b in range(4):
             scaled("s", W("xb", XG + b, XG + 128, 4), W("ps", 512 * b + 96, 512 * b + 128), 1.0 / 64)
         quant(W("qg"), W("sg"), W("xb", XG - 384, XG + 128))
@@ -541,7 +583,7 @@ def rank_program(g, core, T, topo):
             stack_masks()
         for b in range(4):
             mm(4 + b, 128, W("qw", 128 * b, 128 * b + 128), W("sw", 128 * b, 128 * b + 128), W("qg"), W("sg"), False, True)
-        scan(W("ex"), W("cex"), W("i2" if last else "i3"), 0.0, alu.mult, alu.max)
+        scan(W("ex"), W("cex"), W("i2"), 0.0, alu.mult, alu.max)
         for b in range(4):
             scaled("s", W("zz", PL * b + C, PL * b + PL), W("ps", 512 * (4 + b) + 96, 512 * (4 + b) + 128), 1.0 / 32)
         ts(W("offf"), W("ex", 15, C, 16), INV, alu.mult, -1.0, alu.add)
@@ -581,8 +623,4 @@ def rank_program(g, core, T, topo):
             copy(W("ysb", c1, C), W("ps", 512, 512 + C - c1))
             store("y", T.y[:, c1:C], W("ysb", c1, C))
 
-    g.wait_ge(T.sem.sent, sent[0])
-    for q in ENGSEM:
-        learn("y", ENGSEM[q], count[q], {})
-    for i in range(dmas[0]):
-        learn("y", "dma%d" % i, 16, {})
+    emit(plan())

@@ -14,7 +14,7 @@ for _d, _l in (
     (I32, dict(hgi=6, dgi=22, pi=2, pj=2, ti=22, fi=2)),
     (F32, dict(col=16, i32=32, i44=44, sm=64, tab=PL, m16=16, r16=16, x16=48, maskq=C, rst=C, cex=C, bb=C, sc=C, r22=22,
                mm=22, gt=24, ca=8, kp=22, kn=11, k05=16, de=64, dp=32, m3=96, s3=96, ls=96, pm=8, ind=16, eu=32, pr=16,
-               es=16, c4=16, par=8, stp=8, cof=8, dl=8, vc=2, ys=96, cofc=96, ch=96, st1=96, st2=96, st3=96, st4=96,
+               es=16, c4=16, par=8, stp=8, cof=8, dl=8, vc=2, nk=2, ys=96, cofc=96, ch=96, st1=96, st2=96, st3=96, st4=96,
                yi=24, yb=24, ef=24, cl=22, vv=22, eq=22, wm=22, mf=22, bi=22, bm=22, d1=22, d2=22, d3=22, d4=22, d5=22,
                d6=22, i1=PL, i2=C, i3=C, ex=C, hf=8, ho=32, ht=32, ysb=C)),
     (U16, dict(offp=44, offq=22, offu=8, offn=22, offa=8, off3=6, offs=6, offc=6, offe=24, offd=22, offo=22, offm=22,
@@ -95,6 +95,7 @@ def rank_program(g, core, T, topo):
 
     touched = {}
     ops = []
+    fence = []
     loads = {q: [] for q in queue}
 
     def width(v):
@@ -118,6 +119,7 @@ def rank_program(g, core, T, topo):
         if dma and not reads:
             order.update(loads[q][-1:])
             loads[q].append(len(ops))
+        order.update(fence)
         ops.append(dict(q=q, call=call, need=need, order=order - need, cost=cost, dma=dma, far=far))
         for views, wr in ((reads, False), (writes, True)):
             for v in views:
@@ -255,9 +257,6 @@ def rank_program(g, core, T, topo):
     def scan(o, d0, d1, init, op0, op1):
         issue("v", lambda: g.vector.tensor_tensor_scan(ap(o), ap(d0), ap(d1), init, op0, op1), [d0, d1], [o], took("v", d0))
 
-    def reduce(o, i, op):
-        issue("v", lambda: g.vector.tensor_reduce(ap(o), ap(i), AxisListType.X, op), [i], [o], took("v", i))
-
     def quant(q, s, i):
         issue("v", lambda: g.vector.quantize_mx(ap(q), ap(s), ap(i)), [i], [q, s], 12 + 0.22 * width(i))
 
@@ -317,7 +316,7 @@ def rank_program(g, core, T, topo):
     iota(W("pi"), [[0, 2]], 0, 1)
     iota(W("i32"), [[0, 2], [1, 16]])
     iota(W("i44"), [[4, 11], [176, 4]])
-    iota(W("sm", 0, 8), [[704, 2], [1, 4]], -64)
+    iota(W("sm", 0, 8), [[704, 2], [1, 4]])
     iota(W("sm", 8, 14), [[0, 3], [176, 2]], 15)
     iota(W("sm", 18, 24), [[4, 2], [0, 3]])
     iota(W("sm", 24, 46), [[176, 2], [1, 11]])
@@ -325,7 +324,6 @@ def rank_program(g, core, T, topo):
     iota(W("bi"), [[16, 22]])
     iota(W("eu"), [[0, 32]])
     iota(W("eu", 2, 32, 4), [[0, 8]], V)
-    iota(W("gt"), [[0, 24]], 1)
     iota(W("kp"), [[0, 2], [1, 11]], 1)
     iota(W("kn"), [[-1, 11]], -1)
     iota(W("ind"), [[0, 16]])
@@ -412,6 +410,7 @@ def rank_program(g, core, T, topo):
         tt(W("zz", PL * k, PL * k + C), (W("xp", C * k, C * k + C), W("offm")), W("xb", XX + k, XG, 4), alu.add)
 
     K1 = [one("cof", 4 * h + 1) for h in range(2)]
+    NK = [one("nk", h) for h in range(2)]
     NN = [one("par", 4 * h) for h in range(2)]
     EA = [one("es", 4 * h + 3) for h in range(2)]
     EL = [one("es", 8 + 4 * h + 3) for h in range(2)]
@@ -490,11 +489,12 @@ def rank_program(g, core, T, topo):
         eu = W("eu", 8 * t, 8 * t + 8)
         scan(W("mm"), W("r22"), W("sc", 15, C, 16), 0.0, alu.max, alu.min)
         for h in range(2):
-            ts(W("gt", 12 * h + 1, 12 * h + 12), W("mm", 11 * h, 11 * h + 11), one("mm", 11 * h + 10), alu.is_gt)
+            o, i, m = W("gt", 11 * h, 11 * h + 11), W("mm", 11 * h, 11 * h + 11), one("mm", 11 * h + 10)
+            issue("s", lambda o=o, i=i, m=m, k=NK[h]: g.scalar.activation(ap(o), ap(i), act.Sign, bias=ap(m), scale=-1.0,
+                                                                          accum_out=ap(k)), [i], [o, NK[h]], 145)
         for h in range(2):
-            reduce(K1[h], W("gt", 12 * h, 12 * h + 12), alu.add)
-        for h in range(2):
-            ts(W("offa", h, 8, 2), W("ca", 4 * h, 4 * h + 4), K1[h], alu.add, 64.0, alu.mult)
+            ts(W("offa", h, 8, 2), W("ca", 4 * h, 4 * h + 4), NK[h], alu.subtract, 64.0, alu.mult)
+        ts(pair("cof", 1), W("nk"), -1.0, alu.mult, 1.0, alu.add)
         tt(W("s3"), (W("sc"), W("off3")), W("m3"), alu.add)
         for k in (2, 0, 3, 1):
             moved("v" if k < 2 else "s", W("xb", XA + k, XA + 128, 4), (XW, W("offa", 2 * k, 2 * k + 2)))
@@ -503,7 +503,7 @@ def rank_program(g, core, T, topo):
         send(t)
         plane(3)
         for h in range(2):
-            ts(W("ind", 4 * h + 1, 4 * h + 3), W("eu", 8 * t + 4 * h, 8 * t + 4 * h + 2), K1[h], alu.is_lt)
+            ts(W("ind", 4 * h + 1, 4 * h + 3), W("eu", 8 * t + 4 * h, 8 * t + 4 * h + 2), NK[h], alu.add, 0.0, alu.is_le)
         if t == 0:
             issue("g", lambda: g.affine_select(T.et[:], T.c64[:], [[-1, 516]], alu.is_equal, 0.0, 3, 4), [W("c64")],
                   [W("et")], 1200)
@@ -519,14 +519,16 @@ def rank_program(g, core, T, topo):
         tt(W("dl"), W("ind", 0, 8), W("ind", 8, 16), alu.subtract)
         scan(W("es"), W("c4"), W("pr"), 0.0, alu.mult, alu.max)
         tt(pair("par", 0), pair("es", 3), pair("cof", 1), alu.subtract)
-        tt(pair("par", 3), pair("es", 11), pair("es", 3), alu.is_ge)
+        for h in range(2):
+            ts(one("par", 4 * h + 3), one("dl", 4 * h + 1), one("dl", 4 * h + 2), alu.add, 0.0, alu.is_lt)
         moved("s", pair("cof", 2), pair("es", 3))
         for h in range(2):
             activ(one("vc", h), EL[h], act.Identity, NE[h])
         for h in range(2):
             activ(W("vv", 11 * h, 11 * h + 11), W("kn"), act.Identity, NE[h], one("vc", h))
         ts(W("cl", 0, 11), W("kp", 0, 11), K1[0], alu.max, EA[0], alu.min)
-        tt(pair("par", 1), pair("par", 0), pair("par", 3), alu.mult)
+        for h in range(2):
+            ts(one("par", 4 * h + 1), EA[h], K1[h], alu.subtract, one("par", 4 * h + 3), alu.mult)
         ts(W("cl", 11, 22), W("kp", 0, 11), K1[1], alu.max, EA[1], alu.min)
         tt(pair("stp", 2), pair("es", 11), pair("par", 1), alu.subtract)
         tt(pair("stp", 1), pair("es", 3), pair("par", 1), alu.subtract)
@@ -539,7 +541,8 @@ def rank_program(g, core, T, topo):
         if not last:
             end_gaps(t + 1)
         tt(W("st1"), (W("stp"), W("offs")), W("ys"), alu.is_le)
-        tt(pair("cof", 0), pair("cof", 3), pair("par", 0), alu.add)
+        for h in range(2):
+            ts(one("cof", 4 * h), one("stp", 4 * h + 1), one("stp", 4 * h + 2), alu.add, NN[h], alu.add)
         tt(W("eq"), W("cl"), W("kp"), alu.is_equal)
         tt(W("st2"), (W("cof"), W("offc")), W("cofc"), alu.add)
         tt(W("wm"), W("eq"), W("vv"), alu.mult)
@@ -570,20 +573,22 @@ def rank_program(g, core, T, topo):
             for gg in range(8):
                 a, e = gg // 2, gg % 2
                 store("y", T.oh[gg:gg + 1, :], W("ht", 16 * e, 16 * e + 16, 1, 32 * a, 32 * a + 6))
-        both(3)
         for b in range(4):
             mm(b, 128, W("qe", 128 * b, 128 * b + 128), W("se", 128 * b, 128 * b + 128), W(qa, 32, 160), W(sa, 32, 160), far=t)
         for b in range(4):
             mm(4 + b, 128, W("qe", 128 * b, 128 * b + 128), W("se", 128 * b, 128 * b + 128), W(qa, 32, 160), W(sa, 32, 160),
                True, False, far=t)
         for b in range(4):
-            scaled("s", W("xb", XG + b, XG + 128, 4), W("ps", 512 * b + 96, 512 * b + 128), 1.0 / 64)
+            scaled("s" if b < 3 else "v", W("xb", XG + b, XG + 128, 4), W("ps", 512 * b + 96, 512 * b + 128), 1.0 / 64)
         quant(W("qg"), W("sg"), W("xb", XG - 384, XG + 128))
+        fence.append(len(ops) - 1)
+        scan(W("ex"), W("cex"), W("i2"), 0.0, alu.mult, alu.max)
+        both(3)
+        fence.pop()
         if not last:
             stack_masks()
         for b in range(4):
             mm(4 + b, 128, W("qw", 128 * b, 128 * b + 128), W("sw", 128 * b, 128 * b + 128), W("qg"), W("sg"), False, True)
-        scan(W("ex"), W("cex"), W("i2"), 0.0, alu.mult, alu.max)
         for b in range(4):
             scaled("s", W("zz", PL * b + C, PL * b + PL), W("ps", 512 * (4 + b) + 96, 512 * (4 + b) + 128), 1.0 / 32)
         ts(W("offf"), W("ex", 15, C, 16), INV, alu.mult, -1.0, alu.add)

@@ -3,28 +3,39 @@ from concourse.mybir import dt, AluOpType, AxisListType, ActivationFunctionType
 
 C, V, B, ROUNDS = 352, 11, 32, 3
 XA, XX, XG = 0, 128, 128 + 4 * C
-PL = C + B
+HALF, PL = C // 2, C + B
 BIG, TOP = 2.0 ** 90, 2.0 ** 80
 F32, BF, I32, U16, CODE, PLANE = "float32", "bfloat16", "int32", "uint16", "float8_e4m3fn_x4", "uint8"
 SCRATCH = {"ps": ("psum", [128, 4096], F32)}
 for _d, _l in (
-    (BF, dict(xin=4 * C, xb=XG + 128, zz=4 * PL, xp=4 * C, ub=512, vb=512, et=516, c64=516)),
+    (BF, dict(xc=4 * C, xb0=XG + 128, xb1=XG + 128, zz=4 * PL, ub=512, vb=512, et=516, c64=516)),
     (CODE, dict(qu=128, qur=128, qv=128, qw=512, qe=512, qx=C, qg=128, qa0=160, qa1=160, qa2=160)),
     (PLANE, dict(su=128, sur=128, sv=128, sw=512, se=512, sx=C, sg=128, sa0=256, sa1=256, sa2=256)),
-    (I32, dict(hgi=6, dgi=22, pi=2, pj=2, ti=22, fi=2)),
-    (F32, dict(col=16, i32=32, i44=44, sm=64, tab=PL, m16=16, r16=16, x16=48, maskq=C, rst=C, cex=C, bb=C, sc=C, r22=22,
-               mm=22, gt=24, ca=8, kp=22, kn=11, k05=16, de=64, dp=32, m3=96, s3=96, ls=96, pm=8, ind=16, eu=32, pr=16,
-               es=16, c4=16, par=8, stp=8, cof=8, dl=8, vc=2, nk=2, ys=96, cofc=96, ch=96, st1=96, st2=96, st3=96, st4=96,
-               yi=24, yb=24, ef=24, cl=22, vv=22, eq=22, wm=22, mf=22, bi=22, bm=22, d1=22, d2=22, d3=22, d4=22, d5=22,
-               d6=22, i1=PL, i2=C, i3=C, ex=C, hf=8, ho=32, ht=32, ysb=C)),
-    (U16, dict(offp=44, offq=22, offu=8, offn=22, offa=8, off3=6, offs=6, offc=6, offe=24, offd=22, offo=22, offm=22,
-               offf=22)),
+    (I32, dict(hgi=6, dgi=22, pi=1, pj=2, ti=22)),
+    (F32, dict(col=16, i32=32, i22=22, sm=64, tab=2 * C, i44=44, m16=16, r16=16, x16=48, maskq=C, rst=C, cex=C, bb=C, sc=C,
+               pn=C, r22=11, mm=22, ca=16, kn=11, k05=16, de=64, dp=32, m3=96, s3=96, ls=96, ne=16, hh=10, fl=20, pr=36, jj=4,
+               nn=2, nu=2, th=6, eb=154, ec=154, es=154, mb=110, md=110, ms=110, uu=10, uo=10, w1=2, pp=4, d1=22, d2=22, d3=22,
+               d4=22, d5=22, d6=22, i1=C, i2=C, i3=C, ex=C, hf=8, ho=32, ht=32, ysb=C)),
+    (U16, dict(offp=44, offq=22, offu=8, offn=22, offa=8, off3=6, offe=22, offd=22, offo=22, offm=88, offf=22)),
 ):
     for _n, _w in _l.items():
         SCRATCH[_n] = ("sbuf", [128, _w], _d)
 
-WAKE, FAR, ISSUE, SLACK = 150, 4000, 60, 60
-NDMA = 26
+CUT, LASTCUT = 176, 224
+AENG, GENG, HENG = "ssss", "ssss", "ssss"
+ONS = "vvvvvv"
+SORT = "ssvs"
+DEAL = [[("s", 0, 0, 22), ("s", 1, 0, 22), ("v", 2, 0, 22), ("v", 3, 0, 22)],
+        [(q, k, s0, s1) for (s0, s1), qs in (((0, 14), "svsv"), ((14, 22), "ssvs")) for k, q in enumerate(qs)]]
+ORDER = {
+    ("v", 0): "C64 Q MASKS U0 TABLES D N U D2 HEIGHTS SMALL QX0 PREP P QX1 GAPS HIDE0 OWN0 HIDE1 low0 OWN1 low1 s3 ls offa na a1 nf FULL enda endl ends n qa jj nq nu sort2 terms E64 es ms late offm offe listo offm0 both2 both0 both1 ex qg gaps offf both3 deal2 deal3 high qx0 qx1 full hide0 hide1 own0 own1",
+    ("v", 1): "low0 low1 s3 ls offa na a1 nf enda endl n qa nq nu jj ends ms terms late es offm offe offm0 both1 both2 both0 ex qg high offf both3 deal2 deal3 gaps qx0 qx1 full hide0 hide1 own0 own1",
+    ("v", 2): "low0 low1 s3 ls offa na nf a1 enda endl n qa nq nu jj ends ms terms offm0 es offm offe both0 both2 both1 ex qg next offf both3 deal1 deal3 qx0 deal6 qx1 out1",
+    ("s", 0): "LOAD MASKS CEX U HEIGHTS HIGH GAPS COPY0 STACKS COPY1 TAB sign I2 ga x I3 th vv ramps FULL sort0 sort1 sort3 next i1 gaps i2 g stacks h0 h1 h2 h3 deal1 deal0 high full",
+    ("s", 1): "sign ga x vv th ramps next i1 i2 g gaps h0 h1 h2 h3 deal0 deal1 high stacks full",
+    ("s", 2): "sign ga x vv th ramps next i1 i2 g h0 h1 h2 h3 deal0 deal2 deal4 deal7 deal5 out0 scales",
+}
+NDMA = 30
 ENGSEM = {"v": "cv", "s": "cs", "p": "cp", "g": "cg"}
 SEMAPHORES = ["cv", "cs", "cp", "cg", "sent"] + ["arr%d" % t for t in range(ROUNDS)] + ["dma%d" % i for i in range(NDMA)]
 
@@ -74,34 +85,33 @@ def rank_program(g, core, T, topo):
     queue = {"v": g.vector, "s": g.scalar, "p": g.tensor, "g": g, "y": g.sync}
     alu, act = AluOpType, ActivationFunctionType
 
-    def W(name, a=0, b=None, step=1, p0=0, p1=128):
-        return (name, a, SCRATCH[name][1][1] if b is None else b, step, p0, p1)
+    def W(name, a=0, b=None, gap=1, p0=0, p1=128):
+        return (name, a, SCRATCH[name][1][1] if b is None else b, gap, p0, p1)
 
     def ap(v):
-        name, a, b, step, p0, p1 = v
+        name, a, b, gap, p0, p1 = v
         rows = slice(p0, p1) if (p0, p1) != (0, 128) else slice(None)
-        return T[name][rows, a:b:step] if step != 1 else T[name][rows, a:b]
+        return T[name][rows, a:b:gap] if gap != 1 else T[name][rows, a:b]
 
     def cover(v):
-        name, a, b, step = v[:4]
+        name, a, b, gap = v[:4]
         if name == "ps":
             return 1 << (a // 512)
-        if step == 1:
+        if gap == 1:
             return ((1 << (b - a)) - 1) << a
         m = 0
-        for i in range(a, b, step):
+        for i in range(a, b, gap):
             m |= 1 << i
         return m
 
-    touched = {}
-    ops = []
-    fence = []
-    loads = {q: [] for q in queue}
+    touched, ops, now = {}, [], [-1, ""]
 
-    def width(v):
-        return 16 * (v[1][2] - v[1][1]) if len(v) == 2 else len(range(v[1], v[2], v[3]))
+    def step(name, t=None):
+        now[1] = name
+        if t is not None:
+            now[0] = t
 
-    def issue(q, call, reads, writes, cost, dma=False, chained=False, far=None):
+    def issue(q, call, reads, writes, dma=False, chained=False, far=None):
         need, order = set(), set()
         for views, wr in ((reads, False), (writes, True)):
             for v in views:
@@ -116,11 +126,9 @@ def rank_program(g, core, T, topo):
                     elif not (wr or wr2):
                         continue
                     need.add(j)
-        if dma and not reads:
-            order.update(loads[q][-1:])
-            loads[q].append(len(ops))
-        order.update(fence)
-        ops.append(dict(q=q, call=call, need=need, order=order - need, cost=cost, dma=dma, far=far))
+        t, name = max(now[0], 0), now[1] if now[0] >= 0 else now[1].upper()
+        place = ORDER[q, t].split().index(name) if (q, t) in ORDER else 0
+        ops.append(dict(q=q, call=call, need=need, order=order, dma=dma, far=far, key=(t, place, len(ops))))
         for views, wr in ((reads, False), (writes, True)):
             for v in views:
                 m = cover(v)
@@ -129,62 +137,12 @@ def rank_program(g, core, T, topo):
                     old[:] = [e for e in old if e[0] & ~m]
                 old.append((m, wr, len(ops) - 1))
 
-    def plan():
-        late = [o["cost"] for o in ops]
-        rest = [0.0] * len(ops)
-        before = []
-        for i, o in enumerate(ops):
-            e = [(j, WAKE) for j in o["need"]] + [(j, ISSUE - late[j] if o["dma"] else 0) for j in o["order"]]
-            if o["far"] is not None:
-                e.append((sends[o["far"]], FAR))
-            before.append(e)
-        for i in range(len(ops) - 1, -1, -1):
-            rest[i] += late[i]
-            for j, w in before[i]:
-                rest[j] = max(rest[j], rest[i] + w)
-        after = [[] for _ in ops]
-        left = [len(e) for e in before]
-        for i, e in enumerate(before):
-            for j, w in e:
-                after[j].append(i)
-        ready = {q: [] for q in queue}
-        for i, o in enumerate(ops):
-            if not left[i]:
-                ready[o["q"]].append(i)
-        free = {q: 0.0 for q in queue}
-        end = [0.0] * len(ops)
-        seq = []
-
-        def start(i):
-            return max([free[ops[i]["q"]]] + [end[j] + w for j, w in before[i]])
-
-        while len(seq) < len(ops):
-            pick = None
-            for q in queue:
-                if not ready[q]:
-                    continue
-                top = max(ready[q], key=lambda i: (rest[i], -i))
-                s = start(top)
-                fit = [i for i in ready[q] if start(i) < s and start(i) + (ISSUE if ops[i]["dma"] else late[i]) <= s + SLACK]
-                if fit:
-                    top = min(fit, key=lambda i: (start(i), -rest[i], i))
-                if pick is None or start(top) < start(pick):
-                    pick = top
-            s, o = start(pick), ops[pick]
-            end[pick] = s + late[pick]
-            free[o["q"]] = s + ISSUE if o["dma"] else end[pick]
-            ready[o["q"]].remove(pick)
-            seq.append(pick)
-            for i in after[pick]:
-                left[i] -= 1
-                if not left[i]:
-                    ready[ops[i]["q"]].append(i)
-        return seq
-
-    def emit(seq):
+    def emit():
         known = {q: {} for q in queue}
         count = {q: 0 for q in ENGSEM}
         mark, dmas = {}, 0
+        line = {q: sorted((i for i, o in enumerate(ops) if o["q"] == q), key=lambda i: ops[i]["key"], reverse=True)
+                for q in queue}
 
         def learn(q, sem, val, clock):
             if known[q].get(sem, 0) >= val:
@@ -195,15 +153,17 @@ def rank_program(g, core, T, topo):
                 if known[q].get(s2, 0) < v2:
                     known[q][s2] = v2
 
-        for i in seq:
+        while any(line.values()):
+            q = [q for q in queue if line[q] and all(j in mark for j in ops[line[q][-1]]["need"] | ops[line[q][-1]]["order"])][0]
+            i = line[q].pop()
             o = ops[i]
-            q = o["q"]
             for sem, val, clock in sorted((mark[j] for j in o["need"]), key=lambda e: -e[1]):
                 learn(q, sem, val, clock)
             if o["far"] is not None:
                 learn(q, "arr%d" % o["far"], arrives, {})
             ins = o["call"]()
             if ins is None:
+                mark[i] = None
                 continue
             if o["dma"]:
                 sem, val = "dma%d" % dmas, 16
@@ -220,11 +180,6 @@ def rank_program(g, core, T, topo):
         for i in range(dmas):
             learn("y", "dma%d" % i, 16, {})
 
-    def took(q, i, per=1.0):
-        if len(i) == 2:
-            return (50 if q == "v" else 65) + 1.3 * width(i)
-        return max(64, width(i) * per) + (0 if q == "v" else 60)
-
     def src(v):
         if len(v) == 2:
             return ap(v[0]).indirect(ap(v[1])), [v[0], v[1]]
@@ -234,37 +189,40 @@ def rank_program(g, core, T, topo):
         return (ap(s), [s]) if isinstance(s, tuple) else (s, [])
 
     def memset(o, c):
-        issue("v", lambda: g.vector.memset(ap(o), c), [], [o], took("v", o, 0.5))
+        issue("v", lambda: g.vector.memset(ap(o), c), [], [o])
 
     def copy(o, i):
         a, r = src(i)
-        issue("v", lambda: g.vector.tensor_copy(ap(o), a), r, [o], took("v", i))
+        issue("v", lambda: g.vector.tensor_copy(ap(o), a), r, [o])
 
     def tt(o, i0, i1, op):
         a, r = src(i0)
-        issue("v", lambda: g.vector.tensor_tensor(ap(o), a, ap(i1), op), r + [i1], [o],
-              took("v", i0, 1.0 if i0[0] == "ps" else 2.0))
+        issue("v", lambda: g.vector.tensor_tensor(ap(o), a, ap(i1), op), r + [i1], [o])
 
     def ts(o, i0, s1, op0, s2=None, op1=None):
         a, r = src(i0)
         x1, r1 = scal(s1)
         x2, r2 = scal(s2)
         if op1 is None:
-            issue("v", lambda: g.vector.tensor_scalar(ap(o), a, x1, None, op0), r + r1, [o], took("v", i0))
+            issue("v", lambda: g.vector.tensor_scalar(ap(o), a, x1, None, op0), r + r1, [o])
         else:
-            issue("v", lambda: g.vector.tensor_scalar(ap(o), a, x1, x2, op0, op1), r + r1 + r2, [o], took("v", i0))
+            issue("v", lambda: g.vector.tensor_scalar(ap(o), a, x1, x2, op0, op1), r + r1 + r2, [o])
 
-    def scan(o, d0, d1, init, op0, op1):
-        issue("v", lambda: g.vector.tensor_tensor_scan(ap(o), ap(d0), ap(d1), init, op0, op1), [d0, d1], [o], took("v", d0))
+    def scan(o, d0, d1, op0, op1):
+        issue("v", lambda: g.vector.tensor_tensor_scan(ap(o), ap(d0), ap(d1), 0.0, op0, op1), [d0, d1], [o])
 
     def quant(q, s, i):
-        issue("v", lambda: g.vector.quantize_mx(ap(q), ap(s), ap(i)), [i], [q, s], 12 + 0.22 * width(i))
+        issue("v", lambda: g.vector.quantize_mx(ap(q), ap(s), ap(i)), [i], [q, s])
 
-    def activ(o, i, func, scale=1.0, bias=0.0):
+    def activ(o, i, func, scale=1.0, bias=0.0, total=None):
         a, r = src(i)
         x, r1 = scal(scale)
         y, r2 = scal(bias)
-        issue("s", lambda: g.scalar.activation(ap(o), a, func, bias=y, scale=x), r + r1 + r2, [o], took("s", i))
+        if total is None:
+            issue("s", lambda: g.scalar.activation(ap(o), a, func, bias=y, scale=x), r + r1 + r2, [o])
+        else:
+            issue("s", lambda: g.scalar.activation(ap(o), a, func, bias=y, scale=x, accum_out=ap(total)), r + r1 + r2,
+                  [o, total])
 
     def scaled(q, o, i, c):
         if q == "v":
@@ -277,149 +235,85 @@ def rank_program(g, core, T, topo):
             copy(o, i)
         else:
             a, r = src(i)
-            issue("s", lambda: g.scalar.activation(ap(o), a, act.Copy), r, [o], took("s", i))
+            issue("s", lambda: g.scalar.activation(ap(o), a, act.Copy), r, [o])
 
     def mm(bank, ncol, wq, ws, xq, xs, start=True, stop=True, far=None):
         o = W("ps", 512 * bank, 512 * bank + ncol)
         issue("p", lambda: g.tensor.matmul_mx(ap(o), ap(wq), ap(ws), ap(xq), ap(xs), start, stop),
-              [wq, ws, xq, xs], [o], ncol + 16, chained=not start, far=far)
+              [wq, ws, xq, xs], [o], chained=not start, far=far)
 
     def iota(o, pattern, base=0, cm=0):
         if SCRATCH[o[0]][2] == I32:
-            issue("g", lambda: g.iota(ap(o), pattern, base, cm), [], [o], 130 + 2 * width(o))
+            issue("g", lambda: g.iota(ap(o), pattern, base, cm), [], [o])
         else:
-            issue("g", lambda: g.iota(ap(o), pattern, base, cm, allow_small_or_imprecise_dtypes=True), [], [o],
-                  130 + 2 * width(o))
+            issue("g", lambda: g.iota(ap(o), pattern, base, cm, allow_small_or_imprecise_dtypes=True), [], [o])
 
-    def load(q, o, i, cost, codes=False, behind=()):
+    def fill(o, c):
+        iota(o, [[0, len(range(o[1], o[2], o[3]))]], c)
+
+    def load(q, o, i, codes=False, behind=()):
         a = ap(o).bitcast(dt.uint8) if codes else ap(o)
-        issue(q, lambda: queue[q].dma_start(a, i), list(behind), [o], cost, dma=True)
+        issue(q, lambda: queue[q].dma_start(a, i), list(behind), [o], dma=True)
 
     def store(q, o, i, codes=False):
         a = ap(i).bitcast(dt.uint8) if codes else ap(i)
-        issue(q, lambda: queue[q].dma_start(o, a), [i], [], 2500, dma=True)
+        issue(q, lambda: queue[q].dma_start(o, a), [i], [], dma=True)
 
     def one(name, j):
         return W(name, j, j + 1)
 
-    def pair(name, j):
-        return W(name, j, j + 5, 4)
+    def pair(name, j, gap=5):
+        return W(name, j, j + gap + 1, gap)
 
-    half = 2 * C
-    load("y", W("ub"), T.u[:], 2500)
-    load("s", W("hgi"), T.hg[:], 2200)
-    load("y", W("xin", 0, half), T.x[:, 0:half], 3100)
-    load("s", W("dgi"), T.dg[:], 2200)
-    load("y", W("xin", half, 2 * half), T.x[:, half:2 * half], 3700)
+    Q, Q11, Q4, QC, INV, Q16, PP = [one("col", j) for j in range(7)]
+    KP, K1, KN = W("i32", 0, 11), W("i32", 1, 12), W("kn")
+    NK = [one("pr", 5 * h) for h in range(2)]
+    NL = [one("pr", 10 + 5 * h) for h in range(2)]
+    NT = [one("pr", 20 + 5 * h) for h in range(2)]
+    NN = [one("nn", h) for h in range(2)]
 
-    Q, Q3, Q11, PP, Q4, QC, INV, FS = [one("col", j) for j in range(8)]
-    iota(W("pi"), [[0, 2]], 0, 1)
-    iota(W("i32"), [[0, 2], [1, 16]])
-    iota(W("i44"), [[4, 11], [176, 4]])
-    iota(W("sm", 0, 8), [[704, 2], [1, 4]])
-    iota(W("sm", 8, 14), [[0, 3], [176, 2]], 15)
-    iota(W("sm", 18, 24), [[4, 2], [0, 3]])
-    iota(W("sm", 24, 46), [[176, 2], [1, 11]])
-    iota(W("yi"), [[176, 2], [16, 12]])
-    iota(W("bi"), [[16, 22]])
-    iota(W("eu"), [[0, 32]])
-    iota(W("eu", 2, 32, 4), [[0, 8]], V)
-    iota(W("kp"), [[0, 2], [1, 11]], 1)
-    iota(W("kn"), [[-1, 11]], -1)
-    iota(W("ind"), [[0, 16]])
-    iota(W("ind", 0, 16, 4), [[0, 4]], 1)
-    iota(W("c4"), [[0, 16]], 1)
-    iota(W("c4", 0, 16, 4), [[0, 4]])
-    iota(W("stp"), [[0, 8]])
-    iota(W("ys"), [[0, 2], [1, 12], [0, 4]])
-    iota(W("ys", 1, 96, 4), [[0, 2], [1, 12]], 1)
-    iota(W("cofc", 1, 96, 4), [[10, 2], [0, 12]], -23)
-    iota(W("cofc", 2, 96, 4), [[10, 2], [0, 12]], -23)
-    iota(W("cofc", 0, 96, 4), [[0, 2], [-2, 12]], -1)
-    iota(W("cofc", 3, 96, 4), [[0, 2], [-2, 12]], -1)
-    iota(W("ch", 1, 96, 2), [[0, 48]], 1)
-    iota(W("ch", 0, 96, 2), [[0, 24], [-1, 2]])
+    def minus(q, o, a, da, x, b, db, y, c, dc, count=2):
+        if q == "v":
+            tt(W(o, a, a + da * (count - 1) + 1, da), W(x, b, b + db * (count - 1) + 1, db), W(y, c, c + dc * (count - 1) + 1, dc),
+               alu.subtract)
+        else:
+            for j in range(count):
+                activ(one(o, a + da * j), one(y, c + dc * j), act.Identity, -1.0, one(x, b + db * j))
 
-    memset(W("c64"), 64.0)
-    memset(W("r16"), -TOP)
-    ts(one("pj", 0), one("pi", 0), 15, alu.bitwise_and)
-    ts(one("pj", 1), one("pi", 1), 3, alu.bitwise_and)
-    memset(W("r16", 0, 1), TOP)
-    copy(W("col", 0, 2), W("pj"))
-    ts(W("offu"), W("i32", 0, 8), 16.0, alu.mult)
-    ts(W("offq"), W("i32", 0, 22), 0.0, alu.mult, Q, alu.add)
-    ts(W("m16"), W("i32", 0, 16), Q, alu.not_equal, BIG, alu.mult)
-    ts(Q11, Q, 11.0, alu.mult)
-    ts(W("x16", 0, 16), W("i32", 0, 16), Q, alu.not_equal)
-    moved("s", W("maskq"), (W("m16"), W("offq")))
-    moved("s", W("rst"), (W("r16"), W("offq")))
-    ts(W("x16", 16, 32), W("i32", 15, 31), Q, alu.is_equal, 1023.0, alu.mult)
-    ts(PP, Q3, -10.0, alu.mult, Q11, alu.add)
-    ts(Q4, Q, 4.0, alu.mult)
-    tt(W("x16", 32, 48), W("x16", 0, 16), W("x16", 16, 32), alu.add)
-    ts(W("offp"), W("i44"), PP, alu.add)
-    memset(W("r22"), -TOP)
-    ts(FS, Q3, 0.5, alu.mult, 0.25, alu.add)
-    ts(W("ca"), W("sm", 0, 8), Q4, alu.add, 1.0 / 64, alu.mult)
-    memset(W("r22", 0, 22, 11), TOP)
-    copy(one("fi", 0), FS)
-    ts(QC, Q, 10.0, alu.min, 16.0, alu.mult)
-    ts(W("k05"), W("i32", 0, 16), 10.0, alu.min, 0.5, alu.add)
-    copy(FS, one("fi", 0))
-    ts(W("off3"), W("sm", 8, 14), QC, alu.add)
-    ts(W("offc"), W("sm", 18, 24), Q3, alu.add)
-    ts(W("offs"), W("sm", 18, 24), FS, alu.add)
-    ts(INV, Q, 15.0, alu.is_equal, 1.0 / 1024, alu.max)
-    ts(W("offn"), W("sm", 24, 46), Q11, alu.add)
-    ts(W("yb"), W("yi"), Q, alu.add, 1.0 / 16, alu.mult)
-    ts(W("bm"), W("bi"), Q, alu.add)
+    def ends(t, e):
+        return pair("ne", 4 * t + e, 2)
 
-    def end_gaps(t):
+    def prepare(t):
+        step("gaps")
         for e in range(2):
             for h in range(2):
-                activ(W("de", 32 * e + 16 * h, 32 * e + 16 * h + 16), W("k05"), act.Identity, -1.0, one("eu", 8 * t + 4 * h + e))
-
-    def stack_masks():
-        activ(W("m3", 0, 32), W("de", 0, 32), act.Relu, -BIG)
-        activ(W("m3", 64, 96), W("de", 32, 64), act.Relu, BIG)
+                activ(W("de", 32 * e + 16 * h, 32 * e + 16 * h + 16), W("k05"), act.Identity, 1.0, one("ne", 4 * t + 2 * h + e))
+        tt(W("dp"), W("de", 0, 32), W("de", 32, 64), alu.mult)
+        step("stacks")
+        activ(W("m3", 0, 32), W("de", 0, 32), act.Relu, BIG)
+        activ(W("m3", 64, 96), W("de", 32, 64), act.Relu, -BIG)
         activ(W("m3", 32, 64), W("dp"), act.Relu, BIG)
+        step("full")
+        for h in range(2):
+            if ONS[5] == "v":
+                ts(one("pp", h), one("ne", 4 * t + 2 * h), one("hh", 5 * h), alu.mult, one("hh", 5 * h + 2), alu.mult)
+            else:
+                activ(one("pp", 2 + h), one("ne", 4 * t + 2 * h), act.Identity, one("hh", 5 * h))
+                activ(one("pp", h), one("hh", 5 * h + 2), act.Identity, one("pp", 2 + h))
+            activ(W("md", 55 * h + 4, 55 * h + 55, 5), W("r16", 1, 12), act.Sign, one("pp", h))
 
-    XW = W("xb", XX, XG)
+    def quant_x(xb, c0, c1):
+        quant(W("qx", c0, c1), W("sx", c0, c1), W(xb, XX + 4 * c0, XX + 4 * c1))
 
-    def quant_x(c0, c1):
-        quant(W("qx", c0, c1), W("sx", c0, c1), W("xb", XX + 4 * c0, XX + 4 * c1))
-
-    def hide(bank, c0, c1):
-        tt(W("bb", c0, c1), W("ps", 512 * bank, 512 * bank + c1 - c0), W("maskq", c0, c1), alu.add)
+    def product(bank, st, c0, c1):
+        mm(bank, c1 - c0, W("q" + st), W("s" + st), W("qx", c0, c1), W("sx", c0, c1))
 
     def own(c0, c1):
-        scan(W("sc", c0, c1), W("rst", c0, c1), W("bb", c0, c1), 0.0, alu.max, alu.min)
-
-    def order_x(q, h, part):
-        a = XX + half * h + C * part
-        moved(q, W("xb", a, a + C), (W("xin", half * h, half * h + half), W("offp", 22 * part, 22 * part + 22)))
-
-    def deal(q, t, s0, s1):
-        scaled(q, W("xb", XX + 64 * s0 + t, XX + 64 * s1, 4),
-               (W("zz", PL * t, PL * t + PL), W("offf", s0, s1)), 0.5)
-
-    def plane(k):
-        moved("s", W("xp", C * k, C * k + C), W("xb", XX + k, XG, 4))
-
-    def both(k):
-        tt(W("zz", PL * k, PL * k + C), (W("xp", C * k, C * k + C), W("offm")), W("xb", XX + k, XG, 4), alu.add)
-
-    K1 = [one("cof", 4 * h + 1) for h in range(2)]
-    NK = [one("nk", h) for h in range(2)]
-    NN = [one("par", 4 * h) for h in range(2)]
-    EA = [one("es", 4 * h + 3) for h in range(2)]
-    EL = [one("es", 8 + 4 * h + 3) for h in range(2)]
-    NE = [one("par", 4 * h + 2) for h in range(2)]
+        scan(W("sc", c0, c1), W("rst", c0, c1), W("bb", c0, c1), alu.max, alu.min)
 
     hs = helpers(core, nxt, T, topo)
     hp = helpers(prv, core, T, topo)
     arrives = sum(len(topo.engines(c, core)) for c in hp) if hp else len(topo.engines(prv, core))
-    sends = []
 
     def send(t):
         qa, sa, arr = "qa%d" % t, "sa%d" % t, T.sem["arr%d" % t]
@@ -437,195 +331,293 @@ def rank_program(g, core, T, topo):
         def call():
             g.remote_dma_fused(trs, local_sem=T.sem.sent)
 
-        sends.append(len(ops))
-        issue("g", call, [W(qa, 0, 32), W(sa, 0, 128)], [], 300)
+        issue("g", call, [W(qa, 0, 32), W(sa, 0, 128)], [])
 
+    step("load")
+    load("s", W("dgi"), T.dg[:])
+    load("s", W("hgi"), T.hg[:])
+    load("y", W("ub"), T.u[:])
+    load("y", W("xb0", XX, XX + 2 * C), T.x[:, 0:2 * C])
+    load("y", W("xb0", XX + 2 * C, XG), T.x[:, 2 * C:4 * C])
+    load("y", W("xc"), T.x[:], behind=[W("xb0", XX, XX + 2 * C)])
+    load("y", W("qw"), T.wc[:], codes=True)
+    load("y", W("sw"), T.ws[:])
+
+    iota(W("pi"), [[0, 1]], 0, 1)
+    iota(W("i32"), [[0, 2], [1, 16]])
+    iota(W("sm", 24, 46), [[176, 2], [1, 11]])
+    step("c64")
+    memset(W("c64"), 64.0)
+    issue("g", lambda: g.affine_select(T.et[:], T.c64[:], [[-1, 516]], alu.is_equal, 0.0, 3, 4), [W("c64")], [W("et")])
+    step("e64")
+    for b in range(4):
+        quant(W("qe", 128 * b, 128 * b + 128), W("se", 128 * b, 128 * b + 128), W("et", 3 - b, 515 - b))
+    iota(W("tab", 0, HALF), [[1, HALF]], 1)
+    iota(W("sm", 0, 8), [[704, 2], [1, 4]])
+    iota(W("sm", 8, 14), [[0, 3], [176, 2]], 15)
+    iota(W("i44"), [[4, 11], [176, 4]])
+    iota(W("i22"), [[1, 22]])
+    for name, parts in (("hh", ((1, 10, 5, 0), (3, 10, 5, -V), (4, 10, 5, 1))), ("fl", ((0, 20, 1, 1), (0, 20, 5, 0))),
+                        ("uu", ((0, 10, 1, -1), (2, 10, 5, 1))),
+                        ("ec", ((0, 154, 1, 1), (0, 154, 7, 0), (1, 154, 7, -1), (2, 154, 7, -2))),
+                        ("md", ((0, 110, 5, 0), (1, 110, 5, -2), (2, 110, 5, 1))), ("mb", ((2, 110, 5, -1), (3, 110, 5, 0)))):
+        for a, b, gap, c in parts:
+            fill(W(name, a, b, gap), c)
+    step("q")
+    memset(W("r16"), -TOP)
+    memset(W("r22"), -TOP)
+    ts(one("pj", 0), W("pi"), 15, alu.bitwise_and)
+    memset(W("r16", 0, 1), TOP)
+    memset(W("r22", 0, 1), TOP)
+    copy(Q, one("pj", 0))
+    step("masks")
+    ts(W("offq"), W("i32", 0, 22), 0.0, alu.mult, Q, alu.add)
+    ts(W("m16"), W("i32", 0, 16), Q, alu.not_equal, BIG, alu.mult)
+    ts(W("x16", 0, 16), W("i32", 0, 16), Q, alu.not_equal)
+    ts(W("x16", 16, 32), W("i32", 15, 31), Q, alu.is_equal, 1023.0, alu.mult)
+    moved("s", W("maskq"), (W("m16"), W("offq")))
+    moved("s", W("rst"), (W("r16"), W("offq")))
+    step("u0")
+    ts(W("offu"), W("i32", 0, 8), 16.0, alu.mult)
+    ts(Q11, Q, 11.0, alu.mult)
+    tt(W("x16", 32, 48), W("x16", 0, 16), W("x16", 16, 32), alu.add)
+    ts(W("k05"), W("i32", 0, 16), 10.0, alu.min, 0.5, alu.add)
+    step("n")
+    ts(W("offn"), W("sm", 24, 46), Q11, alu.add)
+    ts(QC, Q, 10.0, alu.min, 16.0, alu.mult)
+    step("cex")
     moved("s", W("cex"), (W("x16", 32, 48), W("offq")))
-    iota(W("tab"), [[1, PL]], 1)
+    step("small")
+    ts(W("off3"), W("sm", 8, 14), QC, alu.add)
+    ts(W("ca", 0, 8), W("sm", 0, 8), 0.25, alu.mult, Q11, alu.add)
+    ts(W("kn"), W("i32", 0, 11), -1.0, alu.mult)
+    step("p")
+    ts(one("pj", 1), W("pi"), 3, alu.bitwise_and)
+    ts(PP, one("pj", 1), -10.0, alu.mult, Q11, alu.add)
+    ts(W("offp"), W("i44"), PP, alu.add)
+    step("tables")
+    ts(Q16, Q, 1.0 / 16, alu.mult)
+    ts(INV, Q, 15.0, alu.is_equal, 1.0 / 1024, alu.max)
+    ts(W("mb", 4, 110, 5), W("sm", 24, 46), Q11, alu.add, 2.0, alu.mult)
+    for h in range(2):
+        ts(W("eb", 77 * h + 6, 77 * h + 77, 7), KP, Q16, alu.add, 22.0 * h, alu.add)
+    step("tab")
+    activ(W("tab", C, C + HALF), W("tab", 0, HALF), act.Identity, 1.0, float(HALF))
+    for h in range(2):
+        activ(W("tab", C * h + HALF, C * h + C), (W("i32", 0, 16), W("offq", 0, 11)), act.Identity, 1.0, C + 16.0 * h + 1)
+
+    step("d")
     ts(W("d2"), W("dgi"), -5.0, alu.add, 1.0 / V, alu.mult)
-    copy(W("ti"), W("d2"))
     ts(W("d1"), W("dgi"), 16.0, alu.mult)
+    copy(W("ti"), W("d2"))
+    step("d2")
     ts(W("d3"), W("ti"), -175.0, alu.mult)
-    ts(W("d4"), W("ti"), 16.0, alu.is_ge, 176.0, alu.mult)
-    tt(W("d5"), W("d1"), W("d3"), alu.add)
-    tt(W("d6"), W("d5"), W("d4"), alu.add)
-    copy(W("offd"), W("d6"))
-    moved("s", W("i2"), (W("tab"), W("offd")))
-    moved("s", W("i3"), (W("i2"), W("offn")))
-    scan(W("ex"), W("cex"), W("i3"), 0.0, alu.mult, alu.max)
-    ts(W("offo"), W("ex", 15, C, 16), INV, alu.mult, -1.0, alu.add)
+    ts(W("d4"), W("ti"), 16.0, alu.is_ge, 336.0, alu.mult)
+    step("heights")
     copy(W("hf", 0, 6), W("hgi"))
-    copy(pair("eu", 0), W("hf", 0, 2))
-    tt(pair("eu", 1), W("hf", 0, 2), W("hf", 2, 4), alu.add)
-    end_gaps(0)
+    tt(W("d5"), W("d1"), W("d3"), alu.add)
+    activ(ends(0, 0), W("hf", 0, 2), act.Identity, -1.0)
+    activ(ends(0, 1), W("hf", 4, 6), act.Identity, 1.0, -float(V))
+    step("high")
+    moved("s", pair("hh", 0), W("hf", 2, 4))
+    moved("s", pair("hh", 2), W("hf", 4, 6))
+    step("small")
+    tt(W("d6"), W("d5"), W("d4"), alu.add)
+    step("prep")
+    copy(W("offd"), W("d6"))
+    step("i2")
+    moved("s", W("i2"), (W("tab"), W("offd")))
+    step("i3")
+    moved("s", W("i3"), (W("i2"), W("offn")))
+    prepare(0)
+    step("u")
     quant(W("qu"), W("su"), W("ub"))
     issue("v", lambda: g.vector.tensor_copy(T.qur[:, 0:128].bitcast(dt.uint32),
                                             T.qu[:, 0:128].bitcast(dt.uint32).indirect(T.offu[:, 0:8])),
-          [W("qu"), W("offu")], [W("qur")], 220)
+          [W("qu"), W("offu")], [W("qur")])
     moved("s", W("sur"), (W("su"), W("offu")))
-    tt(W("dp"), W("de", 0, 32), W("de", 32, 64), alu.mult)
-    stack_masks()
-    order_x("s", 0, 1)
-    order_x("v", 0, 0)
-    quant_x(0, 176)
-    mm(0, 176, W("qur"), W("sur"), W("qx", 0, 176), W("sx", 0, 176))
-    order_x("s", 1, 1)
-    order_x("v", 1, 0)
-    load("y", W("qw"), T.wc[:], 3000, codes=True, behind=[W("xin")])
-    load("y", W("sw"), T.ws[:], 3200, behind=[W("xin")])
-    load("y", W("vb"), T.v[:], 3600, behind=[W("xin")])
-    quant_x(176, C)
-    mm(1, 176, W("qur"), W("sur"), W("qx", 176, C), W("sx", 176, C))
-    for k in range(3):
-        plane(k)
-    hide(0, 0, 176)
-    own(0, 176)
-    hide(1, 176, C)
-    own(176, C)
+    for h in range(2):
+        c0, c1 = HALF * h, HALF * h + HALF
+        step("qx%d" % h)
+        quant_x("xb0", c0, c1)
+        product(h, "ur", c0, c1)
+        step("copy%d" % h)
+        moved("s", W("pn", c0, c1), W("ps", 512 * h, 512 * h + HALF))
+        step("hide%d" % h)
+        tt(W("bb", c0, c1), (W("pn", c0, c1), W("offn", 0, 11)), W("maskq", c0, c1), alu.add)
+        step("own%d" % h)
+        own(c0, c1)
 
     for t in range(ROUNDS):
         qa, sa = "qa%d" % t, "sa%d" % t
-        last = t == ROUNDS - 1
-        eu = W("eu", 8 * t, 8 * t + 8)
-        scan(W("mm"), W("r22"), W("sc", 15, C, 16), 0.0, alu.max, alu.min)
+        xb, xn = "xb%d" % (t % 2), "xb%d" % (1 - t % 2)
+        first, last = t == 0, t == ROUNDS - 1
+        wide = 4.0 if first else 64.0
         for h in range(2):
-            o, i, m = W("gt", 11 * h, 11 * h + 11), W("mm", 11 * h, 11 * h + 11), one("mm", 11 * h + 10)
-            issue("s", lambda o=o, i=i, m=m, k=NK[h]: g.scalar.activation(ap(o), ap(i), act.Sign, bias=ap(m), scale=-1.0,
-                                                                          accum_out=ap(k)), [i], [o, NK[h]], 145)
-        for h in range(2):
-            ts(W("offa", h, 8, 2), W("ca", 4 * h, 4 * h + 4), NK[h], alu.subtract, 64.0, alu.mult)
-        ts(pair("cof", 1), W("nk"), -1.0, alu.mult, 1.0, alu.add)
-        tt(W("s3"), (W("sc"), W("off3")), W("m3"), alu.add)
-        for k in (2, 0, 3, 1):
-            moved("v" if k < 2 else "s", W("xb", XA + k, XA + 128, 4), (XW, W("offa", 2 * k, 2 * k + 2)))
-        scan(W("ls"), W("rst", 0, 96), W("s3"), 0.0, alu.max, alu.min)
-        quant(W(qa, 0, 128), W(sa, 0, 128), W("xb", XA, XA + 512))
+            step("low%d" % h, t)
+            scan(W("mm", 11 * h, 11 * h + 11), W("r22", 0, 11), W("sc", HALF * h + 15, HALF * h + HALF, 16), alu.max, alu.min)
+            step("sign")
+            activ(W("mb", 55 * h, 55 * h + 55, 5), W("mm", 11 * h, 11 * h + 11), act.Sign, -1.0, one("mm", 11 * h + 10), NK[h])
+            step("offa")
+            a = 4 * h if first else 8 + 4 * h
+            ts(W("offa", h, 8, 2), W("ca", a, a + 4), NK[h], alu.subtract, wide, alu.mult)
+        step("ga")
+        for k in range(4):
+            moved(AENG[k], W(xb, XA + k, XA + 128, 4), (W(xb, XX, XG), W("offa", 2 * k, 2 * k + 2)))
+        step("qa")
+        quant(W(qa, 0, 128), W(sa, 0, 128), W(xb, XA, XA + 512))
         send(t)
-        plane(3)
+        step("s3")
+        tt(W("s3"), (W("sc"), W("off3")), W("m3"), alu.add)
+        step("ls")
+        scan(W("ls"), W("rst", 0, 96), W("s3"), alu.max, alu.min)
         for h in range(2):
-            ts(W("ind", 4 * h + 1, 4 * h + 3), W("eu", 8 * t + 4 * h, 8 * t + 4 * h + 2), NK[h], alu.add, 0.0, alu.is_le)
-        if t == 0:
-            issue("g", lambda: g.affine_select(T.et[:], T.c64[:], [[-1, 516]], alu.is_equal, 0.0, 3, 4), [W("c64")],
-                  [W("et")], 1200)
+            low = [one("ls", 15 + 16 * h + 32 * s) for s in range(3)]
+            step("nf")
+            ts(one("fl", 5 * h + 1), low[1], low[2], alu.max, low[0], alu.is_le)
+            ts(one("fl", 5 * h + 3), low[0], low[1], alu.max, low[2], alu.is_ge)
+            step("na")
+            ts(W("fl", 12 + 5 * h, 14 + 5 * h), W("ne", 4 * t + 2 * h, 4 * t + 2 * h + 2), NK[h], alu.is_lt)
+        step("a1")
+        tt(pair("fl", 2), pair("ls", 15, 16), pair("mm", 10, 11), alu.is_gt)
+        step("enda")
+        scan(W("pr", 16, 26), W("fl", 10, 20), W("hh"), alu.mult, alu.add)
+        step("endl")
+        scan(W("pr", 7, 16), W("fl", 0, 9), W("hh", 0, 9), alu.mult, alu.add)
+        step("n")
+        tt(W("nn"), pair("pr", 0), pair("pr", 20), alu.subtract)
+        step("jj")
+        minus(ONS[0], "jj", 0, 1, "pr", 0, 5, "pr", 10, 5, 4)
+        step("nu")
         for h in range(2):
-            low = W("ls", 15 + 16 * h, 96, 32)
-            scan(W("pm", 4 * h, 4 * h + 3), low, low, -TOP, alu.max, alu.max)
-        tt(W("pr", 0, 8), W("ind", 0, 8), eu, alu.mult)
+            ts(one("nu", h), NL[h], NK[h], alu.is_lt, NN[h], alu.mult)
+        step("nq")
+        minus(ONS[1], "pr", 30, 5, "pr", 10, 5, "nn", 0, 1)
+        step("th")
         for h in range(2):
-            ts(W("ind", 8 + 4 * h + 1, 8 + 4 * h + 3), W("pm", 4 * h, 4 * h + 2), one("pm", 4 * h + 2), alu.is_lt)
-        ts(pair("par", 2), pair("pm", 2), TOP, alu.is_lt, 16.0, alu.mult)
-        tt(pair("ind", 9), pair("ind", 9), pair("ind", 1), alu.is_ge)
-        tt(W("pr", 8, 16), W("ind", 8, 16), eu, alu.mult)
-        tt(W("dl"), W("ind", 0, 8), W("ind", 8, 16), alu.subtract)
-        scan(W("es"), W("c4"), W("pr"), 0.0, alu.mult, alu.max)
-        tt(pair("par", 0), pair("es", 3), pair("cof", 1), alu.subtract)
+            activ(W("th", 3 * h, 3 * h + 3), W("pr", 10 + 5 * h, 36, 10), act.Identity, 1.0, one("nu", h))
         for h in range(2):
-            ts(one("par", 4 * h + 3), one("dl", 4 * h + 1), one("dl", 4 * h + 2), alu.add, 0.0, alu.is_lt)
-        moved("s", pair("cof", 2), pair("es", 3))
-        for h in range(2):
-            activ(one("vc", h), EL[h], act.Identity, NE[h])
-        for h in range(2):
-            activ(W("vv", 11 * h, 11 * h + 11), W("kn"), act.Identity, NE[h], one("vc", h))
-        ts(W("cl", 0, 11), W("kp", 0, 11), K1[0], alu.max, EA[0], alu.min)
-        for h in range(2):
-            ts(one("par", 4 * h + 1), EA[h], K1[h], alu.subtract, one("par", 4 * h + 3), alu.mult)
-        ts(W("cl", 11, 22), W("kp", 0, 11), K1[1], alu.max, EA[1], alu.min)
-        tt(pair("stp", 2), pair("es", 11), pair("par", 1), alu.subtract)
-        tt(pair("stp", 1), pair("es", 3), pair("par", 1), alu.subtract)
-        tt(pair("stp", 0), pair("stp", 2), pair("par", 0), alu.add)
-        tt(pair("cof", 3), pair("stp", 1), pair("stp", 2), alu.add)
-        for h in range(2):
-            for e in range(2):
-                j = 4 * h + e
-                activ(one("eu", 8 * t + 8 + j), one("dl", j + 1), act.Identity, NN[h], one("eu", 8 * t + j))
-        if not last:
-            end_gaps(t + 1)
-        tt(W("st1"), (W("stp"), W("offs")), W("ys"), alu.is_le)
-        for h in range(2):
-            ts(one("cof", 4 * h), one("stp", 4 * h + 1), one("stp", 4 * h + 2), alu.add, NN[h], alu.add)
-        tt(W("eq"), W("cl"), W("kp"), alu.is_equal)
-        tt(W("st2"), (W("cof"), W("offc")), W("cofc"), alu.add)
-        tt(W("wm"), W("eq"), W("vv"), alu.mult)
-        tt(W("st3"), W("st1"), W("st2"), alu.mult)
-        tt(W("mf"), W("wm"), W("bm"), alu.add)
-        scan(W("st4"), W("ch"), W("st3"), 0.0, alu.mult, alu.add)
-        copy(W("offm"), W("mf"))
-        tt(W("ef"), W("st4", 3, 96, 4), W("yb"), alu.add)
-        ts(W("offe"), W("ef"), 16.0, alu.mult)
+            def term(j):
+                return W("eb", 77 * h + j, 77 * h + 77, 7)
+            step("ramps")
+            activ(term(0), KP, act.Relu, 1.0, one("th", 3 * h + 2))
+            activ(term(1), KP, act.Relu, 1.0, one("th", 3 * h))
+            step("terms")
+            ts(term(2), KN, one("th", 3 * h), alu.is_le, one("jj", 2 + h), alu.mult)
+            ts(term(3), KN, one("th", 3 * h + 2), alu.is_le, one("jj", h), alu.mult)
+            ts(term(4), KN, one("th", 3 * h + 1), alu.is_lt, NN[h], alu.mult)
+            ts(term(5), KN, one("th", 3 * h + 1), alu.is_equal, float(V), alu.mult)
+        step("es")
+        scan(W("es"), W("ec"), W("eb"), alu.mult, alu.add)
+        step("offe")
+        ts(W("offe"), W("es", 6, 154, 7), 16.0, alu.mult)
+        if first:
+            step("listo")
+            scan(W("ex"), W("cex"), W("i3"), alu.mult, alu.max)
+            ts(W("offo"), W("ex", 15, C, 16), INV, alu.mult, -1.0, alu.add)
+        step("i1")
         moved("s", W("i1"), (W("tab"), W("offe")))
+        step("i2")
         moved("s", W("i2"), (W("i1"), W("offd" if last else "offo")))
-        both(0)
+        step("ex")
+        scan(W("ex"), W("cex"), W("i2"), alu.mult, alu.max)
+        step("offf")
+        ts(W("offf"), W("ex", 15, C, 16), INV, alu.mult, -1.0, alu.add)
+        for h in range(2):
+            step("x")
+            activ(W("mb", 55 * h + 1, 55 * h + 55, 5), W("k05", 0, 11), act.Sign, 1.0, one("pr", 19 + 5 * h))
+            step("vv")
+            activ(W("md", 55 * h + 3, 55 * h + 55, 5), K1, act.Identity, 1.0, NL[h])
+        step("ms")
+        scan(W("ms"), W("md"), W("mb"), alu.mult, alu.add)
+        for k in range(4):
+            step("offm" if k else "offm0")
+            ts(W("offm", 22 * k, 22 * k + 22), W("ms", 4, 110, 5), wide / 2, alu.mult, float(k), alu.add)
+        if first:
+            for j in range(4):
+                step("sort%d" % j)
+                a = 2 * C * (j // 2)
+                moved(SORT[j], W(xn, XX + C * j, XX + C * j + C), (W("xc", a, a + 2 * C), W("offp", 22 * (j % 2), 22 * (j % 2) + 22)))
+        for k in range(4):
+            step("both%d" % k)
+            tt(W("zz", PL * k, PL * k + C), (W("xc"), W("offm", 22 * k, 22 * k + 22)), W(xn if first else xb, XX + k, XG, 4), alu.add)
+        step("ends")
+        if ONS[2] == "v":
+            scan(W("uo", 0, 8), W("fl", 0, 8), W("uu", 0, 8), alu.mult, alu.add)
+        else:
+            for h in range(2):
+                activ(one("uo", 5 * h), one("fl", 5 * h + 1), act.Identity, one("fl", 5 * h + 2))
+            minus("s", "uo", 2, 5, "fl", 12, 5, "uo", 0, 5)
+        minus(ONS[3], "w1", 0, 1, "fl", 13, 5, "fl", 3, 5)
+        step("next")
+        for h in range(2):
+            j = 4 * t + 2 * h
+            activ(one("ne", j + 4), one("uo", 5 * h + 2), act.Identity, NN[h], one("ne", j))
+            activ(one("ne", j + 5), one("w1", h), act.Identity, NN[h], one("ne", j + 1))
         if not last:
-            tt(W("dp"), W("de", 0, 32), W("de", 32, 64), alu.mult)
-        if last:
-            e3 = 8 * ROUNDS
-            iota(W("ho"), [[0, 32]])
-            moved("s", W("ho", 0, 2), pair("eu", e3))
-            tt(W("ho", 2, 4), pair("eu", e3 + 1), pair("eu", e3), alu.subtract)
-            tt(W("ho", 4, 6), pair("eu", e3 + 2), pair("eu", e3 + 1), alu.subtract)
-        both(1)
-        both(2)
-        if t == 0:
-            for b in range(4):
-                quant(W("qe", 128 * b, 128 * b + 128), W("se", 128 * b, 128 * b + 128), W("et", 3 - b, 515 - b))
-        if last:
-            issue("v", lambda: g.vector.transpose(T.ht[:], T.ho[:]), [W("ho")], [W("ht")], 64)
+            step("high")
+            activ(pair("hh", 2), ends(t + 1, 1), act.Identity, 1.0, float(V))
+            minus(ONS[4], "hh", 0, 5, "ne", 4 * t + 4, 2, "ne", 4 * t + 5, 2)
+            prepare(t + 1)
+        else:
+            activ(W("ho", 0, 2), ends(ROUNDS, 0), act.Identity, -1.0)
+            activ(W("ho", 4, 6), ends(ROUNDS, 1), act.Identity, 1.0, float(V))
+            tt(W("ho", 2, 4), ends(ROUNDS, 0), ends(ROUNDS, 1), alu.subtract)
+            issue("v", lambda: g.vector.transpose(T.ht[:], T.ho[:]), [W("ho")], [W("ht")])
             for gg in range(8):
                 a, e = gg // 2, gg % 2
                 store("y", T.oh[gg:gg + 1, :], W("ht", 16 * e, 16 * e + 16, 1, 32 * a, 32 * a + 6))
+        if first:
+            step("late")
+            fill(W("ho"), 0)
+            ts(Q4, Q, 4.0, alu.mult)
+            ts(W("d4"), W("ti"), 16.0, alu.is_ge, 160.0, alu.mult)
+            ts(W("mb", 4, 110, 5), W("i22"), Q16, alu.add, 2.0, alu.mult)
+            ts(W("ca", 8, 16), W("sm", 0, 8), Q4, alu.add, 1.0 / 64, alu.mult)
+            tt(W("d6"), W("d5"), W("d4"), alu.add)
+            copy(W("offd"), W("d6"))
+            load("y", W("vb"), T.v[:], behind=[W("offf")])
+        if t == 1:
+            step("late")
+            quant(W("qv"), W("sv"), W("vb"))
         for b in range(4):
             mm(b, 128, W("qe", 128 * b, 128 * b + 128), W("se", 128 * b, 128 * b + 128), W(qa, 32, 160), W(sa, 32, 160), far=t)
         for b in range(4):
             mm(4 + b, 128, W("qe", 128 * b, 128 * b + 128), W("se", 128 * b, 128 * b + 128), W(qa, 32, 160), W(sa, 32, 160),
                True, False, far=t)
+        step("g")
         for b in range(4):
-            scaled("s" if b < 3 else "v", W("xb", XG + b, XG + 128, 4), W("ps", 512 * b + 96, 512 * b + 128), 1.0 / 64)
-        quant(W("qg"), W("sg"), W("xb", XG - 384, XG + 128))
-        fence.append(len(ops) - 1)
-        scan(W("ex"), W("cex"), W("i2"), 0.0, alu.mult, alu.max)
-        both(3)
-        fence.pop()
-        if not last:
-            stack_masks()
+            scaled(GENG[b], W(xb, XG + b, XG + 128, 4), W("ps", 512 * b + 96, 512 * b + 128), 1.0 / 64)
+        step("qg")
+        quant(W("qg"), W("sg"), W(xb, XG - 384, XG + 128))
         for b in range(4):
             mm(4 + b, 128, W("qw", 128 * b, 128 * b + 128), W("sw", 128 * b, 128 * b + 128), W("qg"), W("sg"), False, True)
         for b in range(4):
-            scaled("s", W("zz", PL * b + C, PL * b + PL), W("ps", 512 * (4 + b) + 96, 512 * (4 + b) + 128), 1.0 / 32)
-        ts(W("offf"), W("ex", 15, C, 16), INV, alu.mult, -1.0, alu.add)
-        if t == 1:
-            quant(W("qv"), W("sv"), W("vb"))
-        cut = 14 if last else 12
-        c1 = 16 * cut
-        st = (W("qv"), W("sv")) if last else (W("qur"), W("sur"))
-        deal("v", 0, 0, cut)
-        deal("v", 1, 0, cut)
-        deal("s", 3, 0, cut)
-        deal("v", 2, 0, cut)
-        deal("s", 0, cut, 22)
-        quant_x(0, c1)
-        mm(0, c1, st[0], st[1], W("qx", 0, c1), W("sx", 0, c1))
-        deal("s", 1, cut, 22)
-        deal("v", 3, cut, 22)
-        deal("s", 2, cut, 22)
-        if not last:
-            hide(0, 0, c1)
-            quant_x(c1, C)
-            mm(1, C - c1, st[0], st[1], W("qx", c1, C), W("sx", c1, C))
-            for k in range(3):
-                plane(k)
-            own(0, c1)
-            hide(1, c1, C)
-            own(c1, C)
-        else:
-            store("y", T.oc[:, 0:4 * c1], W("qx", 0, c1), codes=True)
-            quant_x(c1, C)
-            mm(1, C - c1, st[0], st[1], W("qx", c1, C), W("sx", c1, C))
-            moved("s", W("ysb", 0, c1), W("ps", 0, c1))
-            store("y", T.oc[:, 4 * c1:4 * C], W("qx", c1, C), codes=True)
-            store("s", T.y[:, 0:c1], W("ysb", 0, c1))
+            step("h%d" % b)
+            scaled(HENG[b], W("zz", PL * b + C, PL * b + PL), W("ps", 512 * (4 + b) + 96, 512 * (4 + b) + 128), 1.0 / 32)
+        for j, (q, k, s0, s1) in enumerate(DEAL[last]):
+            step("deal%d" % j)
+            scaled(q, W(xn, XX + 64 * s0 + k, XX + 64 * s1, 4), (W("zz", PL * k, PL * k + PL), W("offf", s0, s1)), 0.5)
+        cut = LASTCUT if last else CUT
+        for r, (c0, c1) in enumerate(((0, cut), (cut, C))):
+            step("qx%d" % r)
+            quant_x(xn, c0, c1)
+            product(r, "v" if last else "ur", c0, c1)
+            if not last:
+                o, i = W("xc", 4 * c0, 4 * c1), W(xn, XX + 4 * c0, XX + 4 * c1)
+                issue("y", lambda o=o, i=i: g.sync.dma_start(ap(o), ap(i)), [i], [o], dma=True)
+                step("hide%d" % r)
+                tt(W("bb", c0, c1), W("ps", 512 * r, 512 * r + c1 - c0), W("maskq", c0, c1), alu.add)
+                step("own%d" % r)
+                own(c0, c1)
+            else:
+                store("y", T.oc[:, 4 * c0:4 * c1], W("qx", c0, c1), codes=True)
+                step("out%d" % r)
+                moved("sv"[r], W("ysb", c0, c1), W("ps", 512 * r, 512 * r + c1 - c0))
+                store("y", T.y[:, c0:c1], W("ysb", c0, c1))
+        if last:
+            step("scales")
             for k in range(4):
-                store("y" if k < 2 else "s", T.osc[4 * k:4 * k + 4, :], W("sx", 0, C, 1, 32 * k, 32 * k + 4))
-            copy(W("ysb", c1, C), W("ps", 512, 512 + C - c1))
-            store("y", T.y[:, c1:C], W("ysb", c1, C))
+                store("s", T.osc[4 * k:4 * k + 4, :], W("sx", 0, C, 1, 32 * k, 32 * k + 4))
 
-    emit(plan())
+    emit()

from concourse.bass import DstId, RemoteDMATransfer
from concourse.mybir import dt, AluOpType, AxisListType, ActivationFunctionType

C, V, B, ROUNDS = 352, 11, 32, 3
XA, XX, XG = 0, 128, 128 + 4 * C
HALF, PL = C // 2, C + B
BIG, TOP = 2.0 ** 90, 2.0 ** 80
F32, BF, I32, U16, CODE, PLANE = "float32", "bfloat16", "int32", "uint16", "float8_e4m3fn_x4", "uint8"
SCRATCH = {"ps": ("psum", [128, 4096], F32)}
for _d, _l in (
    (BF, dict(xc=4 * C, xb0=XG + 128, xb1=XG + 128, zz=4 * PL, ub=512, vb=512, et=516, c64=516)),
    (CODE, dict(qu=128, qur=128, qv=128, qw=512, qe=512, qx=C, qg=128, qa0=160, qa1=160, qa2=160)),
    (PLANE, dict(su=128, sur=128, sv=128, sw=512, se=512, sx=C, sg=128, sa0=256, sa1=256, sa2=256)),
    (I32, dict(hgi=6, dgi=22, pi=1, pj=2, ti=22)),
    (F32, dict(col=16, i32=32, i22=22, sm=64, tab=2 * C, i44=44, m16=16, r16=16, x16=48, maskq=C, rst=C, cex=C, bb=C, sc=C,
               pn=C, r22=11, mm=22, ca=16, kn=11, k05=16, de=64, dp=32, m3=96, s3=96, ls=96, ne=16, hh=10, fl=20, pr=36, jj=4,
               nn=2, nu=2, th=6, eb=154, ec=154, es=154, mb=110, md=110, ms=110, uu=10, uo=10, w1=2, pp=4, d1=22, d2=22, d3=22,
               d4=22, d5=22, d6=22, i1=C, i2=C, i3=C, ex=C, hf=8, ho=32, ht=32, ysb=C)),
    (U16, dict(offp=44, offq=22, offu=8, offn=22, offa=8, off3=6, offe=22, offd=22, offo=22, offm=88, offf=22)),
):
    for _n, _w in _l.items():
        SCRATCH[_n] = ("sbuf", [128, _w], _d)

CUT, LASTCUT = 176, 224
AENG, GENG, HENG = "ssss", "ssss", "ssss"
ONS = "vvvvvv"
SORT = "ssvs"
DEAL = [[("s", 0, 0, 22), ("s", 1, 0, 22), ("v", 2, 0, 22), ("v", 3, 0, 22)],
        [(q, k, s0, s1) for (s0, s1), qs in (((0, 14), "svsv"), ((14, 22), "ssvs")) for k, q in enumerate(qs)]]
ORDER = {
    ("v", 0): "C64 Q MASKS U0 TABLES D N U D2 HEIGHTS SMALL QX0 PREP P QX1 GAPS HIDE0 OWN0 HIDE1 low0 OWN1 low1 s3 ls offa na a1 nf FULL enda endl ends n qa jj nq nu sort2 terms E64 es ms late offm offe listo offm0 both2 both0 both1 ex qg gaps offf both3 deal2 deal3 high qx0 qx1 full hide0 hide1 own0 own1",
    ("v", 1): "low0 low1 s3 ls offa na a1 nf enda endl n qa nq nu jj ends ms terms late es offm offe offm0 both1 both2 both0 ex qg high offf both3 deal2 deal3 gaps qx0 qx1 full hide0 hide1 own0 own1",
    ("v", 2): "low0 low1 s3 ls offa na nf a1 enda endl n qa nq nu jj ends ms terms offm0 es offm offe both0 both2 both1 ex qg next offf both3 deal1 deal3 qx0 deal6 qx1 out1",
    ("s", 0): "LOAD MASKS CEX U HEIGHTS HIGH GAPS COPY0 STACKS COPY1 TAB sign I2 ga x I3 th vv ramps FULL sort0 sort1 sort3 next i1 gaps i2 g stacks h0 h1 h2 h3 deal1 deal0 high full",
    ("s", 1): "sign ga x vv th ramps next i1 i2 g gaps h0 h1 h2 h3 deal0 deal1 high stacks full",
    ("s", 2): "sign ga x vv th ramps next i1 i2 g h0 h1 h2 h3 deal0 deal2 deal4 deal7 deal5 out0 scales",
}
NDMA = 30
ENGSEM = {"v": "cv", "s": "cs", "p": "cp", "g": "cg"}
SEMAPHORES = ["cv", "cs", "cp", "cg", "sent"] + ["arr%d" % t for t in range(ROUNDS)] + ["dma%d" % i for i in range(NDMA)]


def helpers(src, dst, T, topo):
    if topo.may_write(src, dst):
        return []
    near = [c for c in topo.cores_of(src) if c != src and T.rank_of(c) is None and topo.may_write(c, dst)]
    near.sort(key=lambda c: (topo.die(c) != topo.die(src), c))
    return near[:2]


def bits(engines):
    m = 0
    for e in engines:
        m |= 1 << e
    return m


def relay_program(g, core, T, topo):
    n = len(T.cores)
    for r in range(n):
        src, dst = T.cores[r], T.cores[(r + 1) % n]
        hs = helpers(src, dst, T, topo)
        if core not in hs:
            continue
        rid, pid = topo.addr(dst, core)
        came = len(topo.engines(src, core)) // 2
        eng = topo.engines(core, dst)
        for t in range(ROUNDS):
            g.wait_ge(T.sem["arr%d" % t], came)
            if core == hs[0]:
                piece = T["qa%d" % t][:, 128:160].bitcast(dt.uint8)
            else:
                piece = T["sa%d" % t][:, 128:160]
            g.remote_dma(piece, piece, T.sem["arr%d" % t], T.sem.sent, pid, rid, bits(eng))
        g.wait_ge(T.sem.sent, ROUNDS * len(eng))


def rank_program(g, core, T, topo):
    rank = T.rank_of(core)
    if rank is None:
        relay_program(g, core, T, topo)
        return
    n = len(T.cores)
    nxt, prv = T.cores[(rank + 1) % n], T.cores[(rank - 1) % n]
    queue = {"v": g.vector, "s": g.scalar, "p": g.tensor, "g": g, "y": g.sync}
    alu, act = AluOpType, ActivationFunctionType

    def W(name, a=0, b=None, gap=1, p0=0, p1=128):
        return (name, a, SCRATCH[name][1][1] if b is None else b, gap, p0, p1)

    def ap(v):
        name, a, b, gap, p0, p1 = v
        rows = slice(p0, p1) if (p0, p1) != (0, 128) else slice(None)
        return T[name][rows, a:b:gap] if gap != 1 else T[name][rows, a:b]

    def cover(v):
        name, a, b, gap = v[:4]
        if name == "ps":
            return 1 << (a // 512)
        if gap == 1:
            return ((1 << (b - a)) - 1) << a
        m = 0
        for i in range(a, b, gap):
            m |= 1 << i
        return m

    touched, ops, now = {}, [], [-1, ""]

    def step(name, t=None):
        now[1] = name
        if t is not None:
            now[0] = t

    def issue(q, call, reads, writes, dma=False, chained=False, far=None):
        need, order = set(), set()
        for views, wr in ((reads, False), (writes, True)):
            for v in views:
                m = cover(v)
                for (m2, wr2, j) in touched.get(v[0], []):
                    if not m & m2:
                        continue
                    if v[0] == "ps":
                        if ops[j]["q"] == q and (chained or not (wr or wr2)):
                            order.add(j)
                            continue
                    elif not (wr or wr2):
                        continue
                    need.add(j)
        t, name = max(now[0], 0), now[1] if now[0] >= 0 else now[1].upper()
        place = ORDER[q, t].split().index(name) if (q, t) in ORDER else 0
        ops.append(dict(q=q, call=call, need=need, order=order, dma=dma, far=far, key=(t, place, len(ops))))
        for views, wr in ((reads, False), (writes, True)):
            for v in views:
                m = cover(v)
                old = touched.setdefault(v[0], [])
                if wr:
                    old[:] = [e for e in old if e[0] & ~m]
                old.append((m, wr, len(ops) - 1))

    def emit():
        known = {q: {} for q in queue}
        count = {q: 0 for q in ENGSEM}
        mark, dmas = {}, 0
        line = {q: sorted((i for i, o in enumerate(ops) if o["q"] == q), key=lambda i: ops[i]["key"], reverse=True)
                for q in queue}

        def learn(q, sem, val, clock):
            if known[q].get(sem, 0) >= val:
                return
            queue[q].wait_ge(T.sem[sem], val)
            known[q][sem] = val
            for s2, v2 in clock.items():
                if known[q].get(s2, 0) < v2:
                    known[q][s2] = v2

        while any(line.values()):
            q = [q for q in queue if line[q] and all(j in mark for j in ops[line[q][-1]]["need"] | ops[line[q][-1]]["order"])][0]
            i = line[q].pop()
            o = ops[i]
            for sem, val, clock in sorted((mark[j] for j in o["need"]), key=lambda e: -e[1]):
                learn(q, sem, val, clock)
            if o["far"] is not None:
                learn(q, "arr%d" % o["far"], arrives, {})
            ins = o["call"]()
            if ins is None:
                mark[i] = None
                continue
            if o["dma"]:
                sem, val = "dma%d" % dmas, 16
                dmas += 1
                ins.then_inc(T.sem[sem], 16)
            else:
                count[q] += 1
                sem, val = ENGSEM[q], count[q]
                ins.then_inc(T.sem[sem], 1)
            mark[i] = (sem, val, dict(known[q]))
        g.wait_ge(T.sem.sent, ROUNDS * len(topo.engines(core, hs[0] if hs else nxt)))
        for q in ENGSEM:
            learn("y", ENGSEM[q], count[q], {})
        for i in range(dmas):
            learn("y", "dma%d" % i, 16, {})

    def src(v):
        if len(v) == 2:
            return ap(v[0]).indirect(ap(v[1])), [v[0], v[1]]
        return ap(v), [v]

    def scal(s):
        return (ap(s), [s]) if isinstance(s, tuple) else (s, [])

    def memset(o, c):
        issue("v", lambda: g.vector.memset(ap(o), c), [], [o])

    def copy(o, i):
        a, r = src(i)
        issue("v", lambda: g.vector.tensor_copy(ap(o), a), r, [o])

    def tt(o, i0, i1, op):
        a, r = src(i0)
        issue("v", lambda: g.vector.tensor_tensor(ap(o), a, ap(i1), op), r + [i1], [o])

    def ts(o, i0, s1, op0, s2=None, op1=None):
        a, r = src(i0)
        x1, r1 = scal(s1)
        x2, r2 = scal(s2)
        if op1 is None:
            issue("v", lambda: g.vector.tensor_scalar(ap(o), a, x1, None, op0), r + r1, [o])
        else:
            issue("v", lambda: g.vector.tensor_scalar(ap(o), a, x1, x2, op0, op1), r + r1 + r2, [o])

    def scan(o, d0, d1, op0, op1):
        issue("v", lambda: g.vector.tensor_tensor_scan(ap(o), ap(d0), ap(d1), 0.0, op0, op1), [d0, d1], [o])

    def quant(q, s, i):
        issue("v", lambda: g.vector.quantize_mx(ap(q), ap(s), ap(i)), [i], [q, s])

    def activ(o, i, func, scale=1.0, bias=0.0, total=None):
        a, r = src(i)
        x, r1 = scal(scale)
        y, r2 = scal(bias)
        if total is None:
            issue("s", lambda: g.scalar.activation(ap(o), a, func, bias=y, scale=x), r + r1 + r2, [o])
        else:
            issue("s", lambda: g.scalar.activation(ap(o), a, func, bias=y, scale=x, accum_out=ap(total)), r + r1 + r2,
                  [o, total])

    def scaled(q, o, i, c):
        if q == "v":
            ts(o, i, c, alu.mult)
        else:
            activ(o, i, act.Identity, c)

    def moved(q, o, i):
        if q == "v":
            copy(o, i)
        else:
            a, r = src(i)
            issue("s", lambda: g.scalar.activation(ap(o), a, act.Copy), r, [o])

    def mm(bank, ncol, wq, ws, xq, xs, start=True, stop=True, far=None):
        o = W("ps", 512 * bank, 512 * bank + ncol)
        issue("p", lambda: g.tensor.matmul_mx(ap(o), ap(wq), ap(ws), ap(xq), ap(xs), start, stop),
              [wq, ws, xq, xs], [o], chained=not start, far=far)

    def iota(o, pattern, base=0, cm=0):
        if SCRATCH[o[0]][2] == I32:
            issue("g", lambda: g.iota(ap(o), pattern, base, cm), [], [o])
        else:
            issue("g", lambda: g.iota(ap(o), pattern, base, cm, allow_small_or_imprecise_dtypes=True), [], [o])

    def fill(o, c):
        iota(o, [[0, len(range(o[1], o[2], o[3]))]], c)

    def load(q, o, i, codes=False, behind=()):
        a = ap(o).bitcast(dt.uint8) if codes else ap(o)
        issue(q, lambda: queue[q].dma_start(a, i), list(behind), [o], dma=True)

    def store(q, o, i, codes=False):
        a = ap(i).bitcast(dt.uint8) if codes else ap(i)
        issue(q, lambda: queue[q].dma_start(o, a), [i], [], dma=True)

    def one(name, j):
        return W(name, j, j + 1)

    def pair(name, j, gap=5):
        return W(name, j, j + gap + 1, gap)

    Q, Q11, Q4, QC, INV, Q16, PP = [one("col", j) for j in range(7)]
    KP, K1, KN = W("i32", 0, 11), W("i32", 1, 12), W("kn")
    NK = [one("pr", 5 * h) for h in range(2)]
    NL = [one("pr", 10 + 5 * h) for h in range(2)]
    NT = [one("pr", 20 + 5 * h) for h in range(2)]
    NN = [one("nn", h) for h in range(2)]

    def minus(q, o, a, da, x, b, db, y, c, dc, count=2):
        if q == "v":
            tt(W(o, a, a + da * (count - 1) + 1, da), W(x, b, b + db * (count - 1) + 1, db), W(y, c, c + dc * (count - 1) + 1, dc),
               alu.subtract)
        else:
            for j in range(count):
                activ(one(o, a + da * j), one(y, c + dc * j), act.Identity, -1.0, one(x, b + db * j))

    def ends(t, e):
        return pair("ne", 4 * t + e, 2)

    def prepare(t):
        step("gaps")
        for e in range(2):
            for h in range(2):
                activ(W("de", 32 * e + 16 * h, 32 * e + 16 * h + 16), W("k05"), act.Identity, 1.0, one("ne", 4 * t + 2 * h + e))
        tt(W("dp"), W("de", 0, 32), W("de", 32, 64), alu.mult)
        step("stacks")
        activ(W("m3", 0, 32), W("de", 0, 32), act.Relu, BIG)
        activ(W("m3", 64, 96), W("de", 32, 64), act.Relu, -BIG)
        activ(W("m3", 32, 64), W("dp"), act.Relu, BIG)
        step("full")
        for h in range(2):
            if ONS[5] == "v":
                ts(one("pp", h), one("ne", 4 * t + 2 * h), one("hh", 5 * h), alu.mult, one("hh", 5 * h + 2), alu.mult)
            else:
                activ(one("pp", 2 + h), one("ne", 4 * t + 2 * h), act.Identity, one("hh", 5 * h))
                activ(one("pp", h), one("hh", 5 * h + 2), act.Identity, one("pp", 2 + h))
            activ(W("md", 55 * h + 4, 55 * h + 55, 5), W("r16", 1, 12), act.Sign, one("pp", h))

    def quant_x(xb, c0, c1):
        quant(W("qx", c0, c1), W("sx", c0, c1), W(xb, XX + 4 * c0, XX + 4 * c1))

    def product(bank, st, c0, c1):
        mm(bank, c1 - c0, W("q" + st), W("s" + st), W("qx", c0, c1), W("sx", c0, c1))

    def own(c0, c1):
        scan(W("sc", c0, c1), W("rst", c0, c1), W("bb", c0, c1), alu.max, alu.min)

    hs = helpers(core, nxt, T, topo)
    hp = helpers(prv, core, T, topo)
    arrives = sum(len(topo.engines(c, core)) for c in hp) if hp else len(topo.engines(prv, core))

    def send(t):
        qa, sa, arr = "qa%d" % t, "sa%d" % t, T.sem["arr%d" % t]
        to = hs if hs else [nxt, nxt]
        eng = topo.engines(core, to[0])
        parts = [eng[:len(eng) // 2], eng[len(eng) // 2:]]
        sides = [(T[qa][:, 0:32].bitcast(dt.uint8), T[qa][:, 128:160].bitcast(dt.uint8)),
                 (T[sa][:, 0:128], T[sa][:, 128:256])]
        trs = []
        for c, e, (a, b) in zip(to, parts, sides):
            rid, pid = topo.addr(c, core)
            trs.append(RemoteDMATransfer(dst_ids=[DstId(rid=rid, pnc=pid)], dma_engine_mask=bits(e), remote_sem=arr,
                                         src=a, dst=b))

        def call():
            g.remote_dma_fused(trs, local_sem=T.sem.sent)

        issue("g", call, [W(qa, 0, 32), W(sa, 0, 128)], [])

    step("load")
    load("s", W("dgi"), T.dg[:])
    load("s", W("hgi"), T.hg[:])
    load("y", W("ub"), T.u[:])
    load("y", W("xb0", XX, XX + 2 * C), T.x[:, 0:2 * C])
    load("y", W("xb0", XX + 2 * C, XG), T.x[:, 2 * C:4 * C])
    load("y", W("xc"), T.x[:], behind=[W("xb0", XX, XX + 2 * C)])
    load("y", W("qw"), T.wc[:], codes=True)
    load("y", W("sw"), T.ws[:])

    iota(W("pi"), [[0, 1]], 0, 1)
    iota(W("i32"), [[0, 2], [1, 16]])
    iota(W("sm", 24, 46), [[176, 2], [1, 11]])
    step("c64")
    memset(W("c64"), 64.0)
    issue("g", lambda: g.affine_select(T.et[:], T.c64[:], [[-1, 516]], alu.is_equal, 0.0, 3, 4), [W("c64")], [W("et")])
    step("e64")
    for b in range(4):
        quant(W("qe", 128 * b, 128 * b + 128), W("se", 128 * b, 128 * b + 128), W("et", 3 - b, 515 - b))
    iota(W("tab", 0, HALF), [[1, HALF]], 1)
    iota(W("sm", 0, 8), [[704, 2], [1, 4]])
    iota(W("sm", 8, 14), [[0, 3], [176, 2]], 15)
    iota(W("i44"), [[4, 11], [176, 4]])
    iota(W("i22"), [[1, 22]])
    for name, parts in (("hh", ((1, 10, 5, 0), (3, 10, 5, -V), (4, 10, 5, 1))), ("fl", ((0, 20, 1, 1), (0, 20, 5, 0))),
                        ("uu", ((0, 10, 1, -1), (2, 10, 5, 1))),
                        ("ec", ((0, 154, 1, 1), (0, 154, 7, 0), (1, 154, 7, -1), (2, 154, 7, -2))),
                        ("md", ((0, 110, 5, 0), (1, 110, 5, -2), (2, 110, 5, 1))), ("mb", ((2, 110, 5, -1), (3, 110, 5, 0)))):
        for a, b, gap, c in parts:
            fill(W(name, a, b, gap), c)
    step("q")
    memset(W("r16"), -TOP)
    memset(W("r22"), -TOP)
    ts(one("pj", 0), W("pi"), 15, alu.bitwise_and)
    memset(W("r16", 0, 1), TOP)
    memset(W("r22", 0, 1), TOP)
    copy(Q, one("pj", 0))
    step("masks")
    ts(W("offq"), W("i32", 0, 22), 0.0, alu.mult, Q, alu.add)
    ts(W("m16"), W("i32", 0, 16), Q, alu.not_equal, BIG, alu.mult)
    ts(W("x16", 0, 16), W("i32", 0, 16), Q, alu.not_equal)
    ts(W("x16", 16, 32), W("i32", 15, 31), Q, alu.is_equal, 1023.0, alu.mult)
    moved("s", W("maskq"), (W("m16"), W("offq")))
    moved("s", W("rst"), (W("r16"), W("offq")))
    step("u0")
    ts(W("offu"), W("i32", 0, 8), 16.0, alu.mult)
    ts(Q11, Q, 11.0, alu.mult)
    tt(W("x16", 32, 48), W("x16", 0, 16), W("x16", 16, 32), alu.add)
    ts(W("k05"), W("i32", 0, 16), 10.0, alu.min, 0.5, alu.add)
    step("n")
    ts(W("offn"), W("sm", 24, 46), Q11, alu.add)
    ts(QC, Q, 10.0, alu.min, 16.0, alu.mult)
    step("cex")
    moved("s", W("cex"), (W("x16", 32, 48), W("offq")))
    step("small")
    ts(W("off3"), W("sm", 8, 14), QC, alu.add)
    ts(W("ca", 0, 8), W("sm", 0, 8), 0.25, alu.mult, Q11, alu.add)
    ts(W("kn"), W("i32", 0, 11), -1.0, alu.mult)
    step("p")
    ts(one("pj", 1), W("pi"), 3, alu.bitwise_and)
    ts(PP, one("pj", 1), -10.0, alu.mult, Q11, alu.add)
    ts(W("offp"), W("i44"), PP, alu.add)
    step("tables")
    ts(Q16, Q, 1.0 / 16, alu.mult)
    ts(INV, Q, 15.0, alu.is_equal, 1.0 / 1024, alu.max)
    ts(W("mb", 4, 110, 5), W("sm", 24, 46), Q11, alu.add, 2.0, alu.mult)
    for h in range(2):
        ts(W("eb", 77 * h + 6, 77 * h + 77, 7), KP, Q16, alu.add, 22.0 * h, alu.add)
    step("tab")
    activ(W("tab", C, C + HALF), W("tab", 0, HALF), act.Identity, 1.0, float(HALF))
    for h in range(2):
        activ(W("tab", C * h + HALF, C * h + C), (W("i32", 0, 16), W("offq", 0, 11)), act.Identity, 1.0, C + 16.0 * h + 1)

    step("d")
    ts(W("d2"), W("dgi"), -5.0, alu.add, 1.0 / V, alu.mult)
    ts(W("d1"), W("dgi"), 16.0, alu.mult)
    copy(W("ti"), W("d2"))
    step("d2")
    ts(W("d3"), W("ti"), -175.0, alu.mult)
    ts(W("d4"), W("ti"), 16.0, alu.is_ge, 336.0, alu.mult)
    step("heights")
    copy(W("hf", 0, 6), W("hgi"))
    tt(W("d5"), W("d1"), W("d3"), alu.add)
    activ(ends(0, 0), W("hf", 0, 2), act.Identity, -1.0)
    activ(ends(0, 1), W("hf", 4, 6), act.Identity, 1.0, -float(V))
    step("high")
    moved("s", pair("hh", 0), W("hf", 2, 4))
    moved("s", pair("hh", 2), W("hf", 4, 6))
    step("small")
    tt(W("d6"), W("d5"), W("d4"), alu.add)
    step("prep")
    copy(W("offd"), W("d6"))
    step("i2")
    moved("s", W("i2"), (W("tab"), W("offd")))
    step("i3")
    moved("s", W("i3"), (W("i2"), W("offn")))
    prepare(0)
    step("u")
    quant(W("qu"), W("su"), W("ub"))
    issue("v", lambda: g.vector.tensor_copy(T.qur[:, 0:128].bitcast(dt.uint32),
                                            T.qu[:, 0:128].bitcast(dt.uint32).indirect(T.offu[:, 0:8])),
          [W("qu"), W("offu")], [W("qur")])
    moved("s", W("sur"), (W("su"), W("offu")))
    for h in range(2):
        c0, c1 = HALF * h, HALF * h + HALF
        step("qx%d" % h)
        quant_x("xb0", c0, c1)
        product(h, "ur", c0, c1)
        step("copy%d" % h)
        moved("s", W("pn", c0, c1), W("ps", 512 * h, 512 * h + HALF))
        step("hide%d" % h)
        tt(W("bb", c0, c1), (W("pn", c0, c1), W("offn", 0, 11)), W("maskq", c0, c1), alu.add)
        step("own%d" % h)
        own(c0, c1)

    for t in range(ROUNDS):
        qa, sa = "qa%d" % t, "sa%d" % t
        xb, xn = "xb%d" % (t % 2), "xb%d" % (1 - t % 2)
        first, last = t == 0, t == ROUNDS - 1
        wide = 4.0 if first else 64.0
        for h in range(2):
            step("low%d" % h, t)
            scan(W("mm", 11 * h, 11 * h + 11), W("r22", 0, 11), W("sc", HALF * h + 15, HALF * h + HALF, 16), alu.max, alu.min)
            step("sign")
            activ(W("mb", 55 * h, 55 * h + 55, 5), W("mm", 11 * h, 11 * h + 11), act.Sign, -1.0, one("mm", 11 * h + 10), NK[h])
            step("offa")
            a = 4 * h if first else 8 + 4 * h
            ts(W("offa", h, 8, 2), W("ca", a, a + 4), NK[h], alu.subtract, wide, alu.mult)
        step("ga")
        for k in range(4):
            moved(AENG[k], W(xb, XA + k, XA + 128, 4), (W(xb, XX, XG), W("offa", 2 * k, 2 * k + 2)))
        step("qa")
        quant(W(qa, 0, 128), W(sa, 0, 128), W(xb, XA, XA + 512))
        send(t)
        step("s3")
        tt(W("s3"), (W("sc"), W("off3")), W("m3"), alu.add)
        step("ls")
        scan(W("ls"), W("rst", 0, 96), W("s3"), alu.max, alu.min)
        for h in range(2):
            low = [one("ls", 15 + 16 * h + 32 * s) for s in range(3)]
            step("nf")
            ts(one("fl", 5 * h + 1), low[1], low[2], alu.max, low[0], alu.is_le)
            ts(one("fl", 5 * h + 3), low[0], low[1], alu.max, low[2], alu.is_ge)
            step("na")
            ts(W("fl", 12 + 5 * h, 14 + 5 * h), W("ne", 4 * t + 2 * h, 4 * t + 2 * h + 2), NK[h], alu.is_lt)
        step("a1")
        tt(pair("fl", 2), pair("ls", 15, 16), pair("mm", 10, 11), alu.is_gt)
        step("enda")
        scan(W("pr", 16, 26), W("fl", 10, 20), W("hh"), alu.mult, alu.add)
        step("endl")
        scan(W("pr", 7, 16), W("fl", 0, 9), W("hh", 0, 9), alu.mult, alu.add)
        step("n")
        tt(W("nn"), pair("pr", 0), pair("pr", 20), alu.subtract)
        step("jj")
        minus(ONS[0], "jj", 0, 1, "pr", 0, 5, "pr", 10, 5, 4)
        step("nu")
        for h in range(2):
            ts(one("nu", h), NL[h], NK[h], alu.is_lt, NN[h], alu.mult)
        step("nq")
        minus(ONS[1], "pr", 30, 5, "pr", 10, 5, "nn", 0, 1)
        step("th")
        for h in range(2):
            activ(W("th", 3 * h, 3 * h + 3), W("pr", 10 + 5 * h, 36, 10), act.Identity, 1.0, one("nu", h))
        for h in range(2):
            def term(j):
                return W("eb", 77 * h + j, 77 * h + 77, 7)
            step("ramps")
            activ(term(0), KP, act.Relu, 1.0, one("th", 3 * h + 2))
            activ(term(1), KP, act.Relu, 1.0, one("th", 3 * h))
            step("terms")
            ts(term(2), KN, one("th", 3 * h), alu.is_le, one("jj", 2 + h), alu.mult)
            ts(term(3), KN, one("th", 3 * h + 2), alu.is_le, one("jj", h), alu.mult)
            ts(term(4), KN, one("th", 3 * h + 1), alu.is_lt, NN[h], alu.mult)
            ts(term(5), KN, one("th", 3 * h + 1), alu.is_equal, float(V), alu.mult)
        step("es")
        scan(W("es"), W("ec"), W("eb"), alu.mult, alu.add)
        step("offe")
        ts(W("offe"), W("es", 6, 154, 7), 16.0, alu.mult)
        if first:
            step("listo")
            scan(W("ex"), W("cex"), W("i3"), alu.mult, alu.max)
            ts(W("offo"), W("ex", 15, C, 16), INV, alu.mult, -1.0, alu.add)
        step("i1")
        moved("s", W("i1"), (W("tab"), W("offe")))
        step("i2")
        moved("s", W("i2"), (W("i1"), W("offd" if last else "offo")))
        step("ex")
        scan(W("ex"), W("cex"), W("i2"), alu.mult, alu.max)
        step("offf")
        ts(W("offf"), W("ex", 15, C, 16), INV, alu.mult, -1.0, alu.add)
        for h in range(2):
            step("x")
            activ(W("mb", 55 * h + 1, 55 * h + 55, 5), W("k05", 0, 11), act.Sign, 1.0, one("pr", 19 + 5 * h))
            step("vv")
            activ(W("md", 55 * h + 3, 55 * h + 55, 5), K1, act.Identity, 1.0, NL[h])
        step("ms")
        scan(W("ms"), W("md"), W("mb"), alu.mult, alu.add)
        for k in range(4):
            step("offm" if k else "offm0")
            ts(W("offm", 22 * k, 22 * k + 22), W("ms", 4, 110, 5), wide / 2, alu.mult, float(k), alu.add)
        if first:
            for j in range(4):
                step("sort%d" % j)
                a = 2 * C * (j // 2)
                moved(SORT[j], W(xn, XX + C * j, XX + C * j + C), (W("xc", a, a + 2 * C), W("offp", 22 * (j % 2), 22 * (j % 2) + 22)))
        for k in range(4):
            step("both%d" % k)
            tt(W("zz", PL * k, PL * k + C), (W("xc"), W("offm", 22 * k, 22 * k + 22)), W(xn if first else xb, XX + k, XG, 4), alu.add)
        step("ends")
        if ONS[2] == "v":
            scan(W("uo", 0, 8), W("fl", 0, 8), W("uu", 0, 8), alu.mult, alu.add)
        else:
            for h in range(2):
                activ(one("uo", 5 * h), one("fl", 5 * h + 1), act.Identity, one("fl", 5 * h + 2))
            minus("s", "uo", 2, 5, "fl", 12, 5, "uo", 0, 5)
        minus(ONS[3], "w1", 0, 1, "fl", 13, 5, "fl", 3, 5)
        step("next")
        for h in range(2):
            j = 4 * t + 2 * h
            activ(one("ne", j + 4), one("uo", 5 * h + 2), act.Identity, NN[h], one("ne", j))
            activ(one("ne", j + 5), one("w1", h), act.Identity, NN[h], one("ne", j + 1))
        if not last:
            step("high")
            activ(pair("hh", 2), ends(t + 1, 1), act.Identity, 1.0, float(V))
            minus(ONS[4], "hh", 0, 5, "ne", 4 * t + 4, 2, "ne", 4 * t + 5, 2)
            prepare(t + 1)
        else:
            activ(W("ho", 0, 2), ends(ROUNDS, 0), act.Identity, -1.0)
            activ(W("ho", 4, 6), ends(ROUNDS, 1), act.Identity, 1.0, float(V))
            tt(W("ho", 2, 4), ends(ROUNDS, 0), ends(ROUNDS, 1), alu.subtract)
            issue("v", lambda: g.vector.transpose(T.ht[:], T.ho[:]), [W("ho")], [W("ht")])
            for gg in range(8):
                a, e = gg // 2, gg % 2
                store("y", T.oh[gg:gg + 1, :], W("ht", 16 * e, 16 * e + 16, 1, 32 * a, 32 * a + 6))
        if first:
            step("late")
            fill(W("ho"), 0)
            ts(Q4, Q, 4.0, alu.mult)
            ts(W("d4"), W("ti"), 16.0, alu.is_ge, 160.0, alu.mult)
            ts(W("mb", 4, 110, 5), W("i22"), Q16, alu.add, 2.0, alu.mult)
            ts(W("ca", 8, 16), W("sm", 0, 8), Q4, alu.add, 1.0 / 64, alu.mult)
            tt(W("d6"), W("d5"), W("d4"), alu.add)
            copy(W("offd"), W("d6"))
            load("y", W("vb"), T.v[:], behind=[W("offf")])
        if t == 1:
            step("late")
            quant(W("qv"), W("sv"), W("vb"))
        for b in range(4):
            mm(b, 128, W("qe", 128 * b, 128 * b + 128), W("se", 128 * b, 128 * b + 128), W(qa, 32, 160), W(sa, 32, 160), far=t)
        for b in range(4):
            mm(4 + b, 128, W("qe", 128 * b, 128 * b + 128), W("se", 128 * b, 128 * b + 128), W(qa, 32, 160), W(sa, 32, 160),
               True, False, far=t)
        step("g")
        for b in range(4):
            scaled(GENG[b], W(xb, XG + b, XG + 128, 4), W("ps", 512 * b + 96, 512 * b + 128), 1.0 / 64)
        step("qg")
        quant(W("qg"), W("sg"), W(xb, XG - 384, XG + 128))
        for b in range(4):
            mm(4 + b, 128, W("qw", 128 * b, 128 * b + 128), W("sw", 128 * b, 128 * b + 128), W("qg"), W("sg"), False, True)
        for b in range(4):
            step("h%d" % b)
            scaled(HENG[b], W("zz", PL * b + C, PL * b + PL), W("ps", 512 * (4 + b) + 96, 512 * (4 + b) + 128), 1.0 / 32)
        for j, (q, k, s0, s1) in enumerate(DEAL[last]):
            step("deal%d" % j)
            scaled(q, W(xn, XX + 64 * s0 + k, XX + 64 * s1, 4), (W("zz", PL * k, PL * k + PL), W("offf", s0, s1)), 0.5)
        cut = LASTCUT if last else CUT
        for r, (c0, c1) in enumerate(((0, cut), (cut, C))):
            step("qx%d" % r)
            quant_x(xn, c0, c1)
            product(r, "v" if last else "ur", c0, c1)
            if not last:
                o, i = W("xc", 4 * c0, 4 * c1), W(xn, XX + 4 * c0, XX + 4 * c1)
                issue("y", lambda o=o, i=i: g.sync.dma_start(ap(o), ap(i)), [i], [o], dma=True)
                step("hide%d" % r)
                tt(W("bb", c0, c1), W("ps", 512 * r, 512 * r + c1 - c0), W("maskq", c0, c1), alu.add)
                step("own%d" % r)
                own(c0, c1)
            else:
                store("y", T.oc[:, 4 * c0:4 * c1], W("qx", c0, c1), codes=True)
                step("out%d" % r)
                moved("sv"[r], W("ysb", c0, c1), W("ps", 512 * r, 512 * r + c1 - c0))
                store("y", T.y[:, c0:c1], W("ysb", c0, c1))
        if last:
            step("scales")
            for k in range(4):
                store("s", T.osc[4 * k:4 * k + 4, :], W("sx", 0, C, 1, 32 * k, 32 * k + 4))

    emit()
